import numpy as np
import ml_dtypes


def mxq(x, axis, fmt="e4m3"):
    dtype, down = {"e4m3": (ml_dtypes.float8_e4m3fn, 7), "e5m2": (ml_dtypes.float8_e5m2, 14)}[fmt]
    v = np.moveaxis(np.asarray(x, np.float32).astype(ml_dtypes.bfloat16).astype(np.float64), axis, -1)
    blocks = v.reshape(v.shape[:-1] + (-1, 32))
    amax = np.abs(blocks).max(-1, keepdims=True)
    byte = np.maximum(np.where(amax > 0, np.frexp(amax)[1] - 1 + 127, 0) - down, 1)
    scale = np.exp2(byte - 127.0)
    codes = (blocks / scale).astype(np.float32).astype(dtype).astype(np.float64)
    return np.moveaxis((codes * scale).reshape(v.shape), -1, axis)


WIDE = False


def mx_kscale(k):
    if not WIDE:
        return np.ones(k)
    levels = np.array([10, -10, 5, -5, 0])
    if k % 512:
        return np.exp2(np.random.permutation(np.resize(levels, k // 32))).repeat(32)
    a = np.empty((k // 512, 16))
    for p in range(k // 512):
        a[p, :8] = np.random.permutation(np.resize(levels, 8))
        for g in range(8):
            far = levels[np.abs(levels - a[p, g]) >= 10]
            a[p, g + 8] = far[np.random.randint(len(far))]
    return np.exp2(a.ravel()).repeat(32)


def f64(x):
    return np.asarray(x).astype(np.float64)


def striped(idx):
    return np.tile(idx.reshape(-1, 16).T, (8, 1)).astype(np.uint16)


def unstriped(offs):
    return offs[:16].T.reshape(-1).astype(np.int64)


E2M1 = np.array([0.0, 0.5, 1.0, 1.5, 2.0, 3.0, 4.0, 6.0, -0.0, -0.5, -1.0, -1.5, -2.0, -3.0, -4.0, -6.0])


def pack_weight(w, fmt):
    k, n = w.shape
    w = f64(np.asarray(w, np.float32).astype(ml_dtypes.bfloat16)).reshape(k // 32, 32, n)
    amax = np.abs(w).max(1)
    if fmt == "e4m3":
        byte = np.frexp(amax)[1] - 1 + 127 - 7
    else:
        mant, ex = np.frexp(amax / 6.0)
        byte = np.where(mant > 0.5, ex, ex - 1) + 127
    byte = np.clip(np.where(amax > 0, byte, 1), 1, 254)
    scaled = (w * np.exp2(127.0 - byte)[:, None, :]).reshape(k, n).astype(np.float32)
    by_word = np.ascontiguousarray(scaled.reshape(k // 512, 128, 4, n).transpose(0, 1, 3, 2))
    if fmt == "e4m3":
        words = by_word.astype(ml_dtypes.float8_e4m3fn).view(np.uint8)
    else:
        c = by_word.astype(ml_dtypes.float4_e2m1fn).view(np.uint8) & 0xF
        words = (c[..., 0::2] | (c[..., 1::2] << 4)).reshape(k // 512, 128, 2 * n)
    return np.ascontiguousarray(words), np.ascontiguousarray(byte.astype(np.uint8).reshape(k // 512, 16, n))


def unpack_weight(words, scales, fmt):
    g, _, n = scales.shape
    words = np.ascontiguousarray(words).reshape(g, 128, n, -1)
    if fmt == "e4m3":
        vals = words.view(ml_dtypes.float8_e4m3fn).astype(np.float64)
    else:
        nib = np.empty((g, 128, n, 4), np.uint8)
        nib[..., 0::2] = words & 0xF
        nib[..., 1::2] = words >> 4
        vals = E2M1[nib]
    vals = vals * np.repeat(np.exp2(scales.astype(np.float64) - 127.0), 8, axis=1)[..., None]
    return vals.transpose(0, 1, 3, 2).reshape(g * 512, n)


def pack_table(v):
    words, scales = pack_weight(v, "e4m3")
    return np.concatenate([words.reshape(words.shape[0], -1), scales.reshape(scales.shape[0], -1)], axis=1)


def unpack_table(tab):
    g, t = tab.shape[0], tab.shape[1] // 528
    return unpack_weight(tab[:, :512 * t].reshape(g, 128, t, 4), tab[:, 512 * t:].reshape(g, 16, t), "e4m3")


def gelu(v):
    return 0.5 * v * (1.0 + np.tanh(np.sqrt(2.0 / np.pi) * (v + 0.044715 * v**3)))


K, M, T, S = 1536, 512, 4096, 2048


def setup_inputs():
    n = np.random.standard_normal
    s = mx_kscale(K)[:, None]
    return {
        "tab": pack_table(n((K, T)) * s),
        "w": (n((K, M)) / np.sqrt(K) / s).astype(np.float32),
        "b": (0.3 * n(512)).astype(np.float32),
        "offs": striped(np.random.permutation(T)[:S]),
    }


def reference(tab, w, b, offs):
    tab_ = unpack_table(tab)[:, unstriped(offs)]
    w_ = mxq(f64(w), 0, "e4m3")
    y = tab_.T @ w_
    return gelu(y + f64(b)[None, :])

@@ -1,0 +1,157 @@
+from contextlib import ExitStack
+
+import concourse.mybir as mybir
+from concourse.masks import make_identity
+
+F32 = mybir.dt.float32
+BF16 = mybir.dt.bfloat16
+I32 = mybir.dt.int32
+U32 = mybir.dt.uint32
+U16 = mybir.dt.uint16
+U8 = mybir.dt.uint8
+FP8X4 = mybir.dt.float8_e4m3fn_x4
+ADD = mybir.AluOpType.add
+MULT = mybir.AluOpType.mult
+GELU = mybir.ActivationFunctionType.Gelu_apprx_tanh
+
+K, N, T, S = 1536, 512, 4096, 2048
+P = 128
+PASSES = K // 512
+H = N // 2
+PAIRS = S // (2 * P)
+FLOPS = 2 * K * N * S
+
+
+def tile_list_tabw_tm_gelu_kernel(tc, tab, w, b, offs, out):
+    nc = tc.nc
+    with ExitStack() as ctx:
+        keep = ctx.enter_context(tc.tile_pool(name="keep", bufs=1))
+        turns = ctx.enter_context(tc.tile_pool(name="turns", bufs=1))
+        stage = ctx.enter_context(tc.tile_pool(name="stage", bufs=8))
+        psum = ctx.enter_context(tc.psum_pool(name="psum", bufs=PAIRS))
+
+        offsets = keep.tile([P, S // 16], U16, name="offsets")
+        planes = keep.tile([P, T], U8, align_bytes=64, name="planes")
+        words = [turns.tile([P, T], I32, align_bytes=64, name="words_even")]
+        words.append(keep.tile([P, T], I32, align_bytes=64, name="words_odd"))
+        w_grp = [keep.tile([P, N, 4], BF16, align_bytes=64, name=f"w_grp{a}") for a in range(PASSES)]
+        w_codes = [keep.tile([P, N], U32, align_bytes=64, name=f"w_codes{a}") for a in range(PASSES)]
+        w_scales = [keep.tile([P, N], U8, align_bytes=64, name=f"w_scales{a}") for a in range(PASSES)]
+        g_words = [keep.tile([P, S], U32, align_bytes=64, name=f"g_words{a}") for a in range(PASSES)]
+        g_planes = keep.tile([P, S], U8, align_bytes=64, name="g_planes")
+        bias = keep.tile([P, 2, 2, H], F32, align_bytes=64, name="bias")
+        b_rows = turns.tile([P, P], F32, align_bytes=64, name="turn0")
+        b_cols = turns.tile([P, N // P], F32, align_bytes=64, name="turn1")
+        ident = turns.tile([P, P], F32, align_bytes=64, name="turn2")
+        warm = keep.tile([P, 1], F32, name="warm")
+
+        nc.gpsimd.memset(b_rows[:], 0.0)
+        nc.vector.memset(planes[:].bitcast(I32), 0)
+        nc.gpsimd.memset(warm[:], 0.0)
+        nc.sync.dma_start(offsets[:], offs)
+        nc.sync.dma_start(out=b_rows[0 : N // P, :], in_=b.rearrange("(c p) -> c p", p=P))
+
+        def load_words(a):
+            nc.sync.dma_start(out=words[a][:], in_=tab[a, 0 : 512 * T].rearrange("(p x) -> p x", p=P).bitcast(I32))
+
+        load_words(0)
+        load_words(1)
+        scale_rows = tab[:, 512 * T : 528 * T].rearrange("a (q t) -> a q t", t=T)
+        for quad in range(4):
+            nc.gpsimd.dma_start(
+                out=planes[32 * quad : 32 * quad + 4 * PASSES, :].bitcast(I32),
+                in_=scale_rows[:, 4 * quad : 4 * quad + 4, :].bitcast(I32),
+            )
+        make_identity(nc, ident[:])
+        nc.scalar.activation(warm[:], warm[:], GELU)
+
+        turned = psum.tile([P, N], F32, name="acc")
+        nc.tensor.transpose(turned[:, 0:P], b_rows[:], ident[:])
+        nc.scalar.copy(b_cols[:], turned[:, 0 : N // P])
+        spread = psum.tile([P, N], F32, name="acc")
+        for c in range(N // P):
+            nc.tensor.transpose(spread[:, P * c : P * (c + 1)], b_cols[:, c : c + 1].to_broadcast([P, P]), ident[:])
+        for u in range(2):
+            nc.scalar.copy(bias[:, :, u, :], spread[:].rearrange("p (h n) -> p h n", h=2))
+
+        def gather_planes():
+            nc.vector.tensor_copy(g_planes[:], planes[:].indirect(offsets[:]))
+
+        def gather_words(a, j0, j1):
+            nc.vector.tensor_copy(g_words[a][:, j0:j1], words[a][:].bitcast(U32).indirect(offsets[:, j0 // 16 : j1 // 16]))
+
+        def pool_copy(dst, src):
+            nc.gpsimd.tensor_scalar(dst, src, 1.0, 0.0, MULT, ADD)
+
+        def prepare(a, h, by_scalar):
+            raw = turns.tile([P, 4, H], F32, align_bytes=64, name=f"turn{a}")
+            nc.sync.dma_start(
+                out=raw[:], in_=w[512 * a : 512 * (a + 1), H * h : H * (h + 1)].rearrange("(p j) n -> p j n", j=4)
+            )
+            for engine_copy, n0, n1 in ((nc.scalar.copy, 0, by_scalar), (pool_copy, by_scalar, H)):
+                engine_copy(
+                    w_grp[a][:, H * h + n0 : H * h + n1, :].rearrange("p (c i) t -> p c t i", i=4),
+                    raw[:, :, n0:n1].rearrange("p t (c i) -> p c t i", i=4),
+                )
+            cols = slice(H * h, H * (h + 1))
+            nc.vector.quantize_mx(
+                out=w_codes[a][:, cols].bitcast(FP8X4),
+                scales=w_scales[a][:, cols],
+                in_=w_grp[a][:, cols, :].rearrange("p n t -> p (n t)"),
+            )
+
+        def multiply(acc, i, h, a):
+            tokens = slice(P * i, P * (i + 1))
+            cols = slice(H * h, H * (h + 1))
+            nc.tensor.matmul_mx(
+                out=acc[:, H * (i % 2) : H * (i % 2 + 1)],
+                lhsT=g_words[a][:, tokens].bitcast(FP8X4),
+                lhsT_scale=g_planes[4 * a : P, tokens],
+                rhs=w_codes[a][:, cols].bitcast(FP8X4),
+                rhs_scale=w_scales[a][:, cols],
+                start=(a == 0),
+                stop=(a == PASSES - 1),
+            )
+
+        def finish(acc, pair, h, tiles):
+            for us in tiles:
+                part = slice(H * us[0], H * (us[-1] + 1))
+                width = H * len(us)
+                summed = stage.tile([P, width], F32, name="summed")
+                nc.vector.tensor_tensor(
+                    summed[:], acc[:, part], bias[:, h, us[0] : us[-1] + 1, :].rearrange("p u n -> p (u n)"), ADD
+                )
+                result = stage.tile([P, width], F32, name="result")
+                nc.scalar.activation(result[:], summed[:], GELU)
+                t0 = 2 * P * pair + P * us[0]
+                nc.sync.dma_start(
+                    out=out[t0 : t0 + P * len(us), H * h : H * (h + 1)].rearrange("(u q) n -> q u n", q=P),
+                    in_=result[:].rearrange("p (u n) -> p u n", n=H),
+                )
+
+        for a in range(PASSES):
+            prepare(a, 0, 208)
+        gather_words(0, 0, S)
+        gather_words(1, 0, S)
+        gather_planes()
+        words.append(turns.tile([P, T], I32, align_bytes=64, name="words_even"))
+        load_words(2)
+        for a in range(PASSES):
+            prepare(a, 1, 160)
+        accs = [psum.tile([P, N], F32, name="acc") for pair in range(PAIRS)]
+        for a in range(PASSES - 1):
+            for pair in range(PAIRS):
+                multiply(accs[pair], 2 * pair, 0, a)
+        for pair in range(PAIRS):
+            if pair % 2 == 0:
+                gather_words(2, 2 * P * pair, 2 * P * (pair + 2))
+            multiply(accs[pair], 2 * pair, 0, PASSES - 1)
+            for a in range(PASSES):
+                multiply(accs[pair], 2 * pair + 1, 0, a)
+            finish(accs[pair], pair, 0, ((0, 1),))
+        for pair in range(PAIRS):
+            acc = psum.tile([P, N], F32, name="acc")
+            for u in range(2):
+                for a in range(PASSES):
+                    multiply(acc, 2 * pair + u, 1, a)
+            finish(acc, pair, 1, ((0, 1),) if pair < PAIRS - 1 else ((0,), (1,)))

@@ -11,14 +11,14 @@ U16 = mybir.dt.uint16
 U8 = mybir.dt.uint8
 FP8X4 = mybir.dt.float8_e4m3fn_x4
 ADD = mybir.AluOpType.add
-MULT = mybir.AluOpType.mult
 GELU = mybir.ActivationFunctionType.Gelu_apprx_tanh
 
 K, N, T, S = 1536, 512, 4096, 2048
 P = 128
 PASSES = K // 512
 H = N // 2
-PAIRS = S // (2 * P)
+TILES = S // P
+BANKS = 8
 FLOPS = 2 * K * N * S
 
 
@@ -26,132 +26,118 @@ def tile_list_tabw_tm_gelu_kernel(tc, tab, w, b, offs, out):
     nc = tc.nc
     with ExitStack() as ctx:
         keep = ctx.enter_context(tc.tile_pool(name="keep", bufs=1))
-        turns = ctx.enter_context(tc.tile_pool(name="turns", bufs=1))
-        stage = ctx.enter_context(tc.tile_pool(name="stage", bufs=8))
-        psum = ctx.enter_context(tc.psum_pool(name="psum", bufs=PAIRS))
+        laid = ctx.enter_context(tc.tile_pool(name="laid", bufs=1))
+        stage = ctx.enter_context(tc.tile_pool(name="stage", bufs=6))
+        psum = ctx.enter_context(tc.psum_pool(name="psum", bufs=BANKS))
 
         offsets = keep.tile([P, S // 16], U16, name="offsets")
         planes = keep.tile([P, T], U8, align_bytes=64, name="planes")
-        words = [turns.tile([P, T], I32, align_bytes=64, name="words_even")]
-        words.append(keep.tile([P, T], I32, align_bytes=64, name="words_odd"))
-        w_grp = [keep.tile([P, N, 4], BF16, align_bytes=64, name=f"w_grp{a}") for a in range(PASSES)]
         w_codes = [keep.tile([P, N], U32, align_bytes=64, name=f"w_codes{a}") for a in range(PASSES)]
         w_scales = [keep.tile([P, N], U8, align_bytes=64, name=f"w_scales{a}") for a in range(PASSES)]
         g_words = [keep.tile([P, S], U32, align_bytes=64, name=f"g_words{a}") for a in range(PASSES)]
         g_planes = keep.tile([P, S], U8, align_bytes=64, name="g_planes")
-        bias = keep.tile([P, 2, 2, H], F32, align_bytes=64, name="bias")
-        b_rows = turns.tile([P, P], F32, align_bytes=64, name="turn0")
-        b_cols = turns.tile([P, N // P], F32, align_bytes=64, name="turn1")
-        ident = turns.tile([P, P], F32, align_bytes=64, name="turn2")
-        warm = keep.tile([P, 1], F32, name="warm")
+        bias = keep.tile([P, N], F32, align_bytes=64, name="bias")
+        b_cols = keep.tile([P, 4], F32, align_bytes=64, name="slot_b")
+        warm = keep.tile([P, 1], F32, align_bytes=64, name="slot_a")
+        words = {}
 
-        nc.gpsimd.memset(b_rows[:], 0.0)
-        nc.vector.memset(planes[:].bitcast(I32), 0)
-        nc.gpsimd.memset(warm[:], 0.0)
-        nc.sync.dma_start(offsets[:], offs)
-        nc.sync.dma_start(out=b_rows[0 : N // P, :], in_=b.rearrange("(c p) -> c p", p=P))
-
-        def load_words(a):
+        def load_words(a, tile):
+            words[a] = tile
             nc.sync.dma_start(out=words[a][:], in_=tab[a, 0 : 512 * T].rearrange("(p x) -> p x", p=P).bitcast(I32))
 
-        load_words(0)
-        load_words(1)
+        def load_w(a, parts, offset):
+            width = N // parts
+            raw = laid.tile([P, parts, 4, width], F32, align_bytes=64, offset=offset, name=f"w_raw{a}")
+            for h in range(parts):
+                nc.sync.dma_start(
+                    out=raw[:, h],
+                    in_=w[512 * a : 512 * (a + 1), width * h : width * (h + 1)].rearrange("(p j) n -> p j n", j=4),
+                )
+            return [raw[:, h] for h in range(parts)]
+
+        def group(raw, engine_copy, name):
+            width = raw.shape[2]
+            grouped = keep.tile([P, width, 4], BF16, align_bytes=64, name=name)
+            engine_copy(
+                grouped[:].rearrange("p (c i) t -> p c t i", i=4),
+                raw.rearrange("p t (c i) -> p c t i", i=4),
+            )
+            return grouped
+
+        def quantise(grouped, a, n0):
+            cols = slice(n0, n0 + grouped.shape[1])
+            nc.vector.quantize_mx(
+                out=w_codes[a][:, cols].bitcast(FP8X4),
+                scales=w_scales[a][:, cols],
+                in_=grouped[:].rearrange("p n t -> p (n t)"),
+            )
+
+        def gather_words(a, j0, j1):
+            nc.vector.tensor_copy(g_words[a][:, j0:j1], words[a][:].bitcast(U32).indirect(offsets[:, j0 // 16 : j1 // 16]))
+
+        def multiply(acc, i, a):
+            tokens = slice(P * i, P * (i + 1))
+            nc.tensor.matmul_mx(
+                out=acc[:],
+                lhsT=g_words[a][:, tokens].bitcast(FP8X4),
+                lhsT_scale=g_planes[4 * a : P, tokens],
+                rhs=w_codes[a][:].bitcast(FP8X4),
+                rhs_scale=w_scales[a][:],
+                start=(a == 0),
+                stop=(a == PASSES - 1),
+            )
+
+        def finish(acc, i, parts):
+            for n0, n1 in parts:
+                summed = stage.tile([P, n1 - n0], F32, name="summed")
+                nc.vector.tensor_tensor(summed[:], acc[:, n0:n1], bias[:, n0:n1], ADD)
+                result = stage.tile([P, n1 - n0], F32, name="result")
+                nc.scalar.activation(result[:], summed[:], GELU)
+                nc.sync.dma_start(out=out[P * i : P * (i + 1), n0:n1], in_=result[:])
+
+        nc.vector.memset(planes[:].bitcast(I32), 0)
+        nc.vector.memset(warm[:], 0.0)
+        nc.sync.dma_start(offsets[:], offs)
+        load_words(0, keep.tile([P, T], I32, align_bytes=64, name="words0"))
+        nc.sync.dma_start(out=b_cols[:], in_=b.rearrange("(p c) -> p c", c=4))
+        raw0 = load_w(0, 1, 12288)
         scale_rows = tab[:, 512 * T : 528 * T].rearrange("a (q t) -> a q t", t=T)
         for quad in range(4):
             nc.gpsimd.dma_start(
                 out=planes[32 * quad : 32 * quad + 4 * PASSES, :].bitcast(I32),
                 in_=scale_rows[:, 4 * quad : 4 * quad + 4, :].bitcast(I32),
             )
-        make_identity(nc, ident[:])
         nc.scalar.activation(warm[:], warm[:], GELU)
-
-        turned = psum.tile([P, N], F32, name="acc")
-        nc.tensor.transpose(turned[:, 0:P], b_rows[:], ident[:])
-        nc.scalar.copy(b_cols[:], turned[:, 0 : N // P])
+        ident = keep.tile([P, P], F32, align_bytes=64, name="slot_a")
+        make_identity(nc, ident[:])
         spread = psum.tile([P, N], F32, name="acc")
-        for c in range(N // P):
+        for c in range(4):
             nc.tensor.transpose(spread[:, P * c : P * (c + 1)], b_cols[:, c : c + 1].to_broadcast([P, P]), ident[:])
-        for u in range(2):
-            nc.scalar.copy(bias[:, :, u, :], spread[:].rearrange("p (h n) -> p h n", h=2))
+        nc.scalar.copy(bias[:].rearrange("p (m c) -> p m c", c=4), spread[:].rearrange("p (c m) -> p m c", c=4))
+        load_words(1, keep.tile([P, T], I32, align_bytes=64, name="slot_b"))
 
-        def gather_planes():
-            nc.vector.tensor_copy(g_planes[:], planes[:].indirect(offsets[:]))
-
-        def gather_words(a, j0, j1):
-            nc.vector.tensor_copy(g_words[a][:, j0:j1], words[a][:].bitcast(U32).indirect(offsets[:, j0 // 16 : j1 // 16]))
-
-        def pool_copy(dst, src):
-            nc.gpsimd.tensor_scalar(dst, src, 1.0, 0.0, MULT, ADD)
-
-        def prepare(a, h, by_scalar):
-            raw = turns.tile([P, 4, H], F32, align_bytes=64, name=f"turn{a}")
-            nc.sync.dma_start(
-                out=raw[:], in_=w[512 * a : 512 * (a + 1), H * h : H * (h + 1)].rearrange("(p j) n -> p j n", j=4)
-            )
-            for engine_copy, n0, n1 in ((nc.scalar.copy, 0, by_scalar), (pool_copy, by_scalar, H)):
-                engine_copy(
-                    w_grp[a][:, H * h + n0 : H * h + n1, :].rearrange("p (c i) t -> p c t i", i=4),
-                    raw[:, :, n0:n1].rearrange("p t (c i) -> p c t i", i=4),
-                )
-            cols = slice(H * h, H * (h + 1))
-            nc.vector.quantize_mx(
-                out=w_codes[a][:, cols].bitcast(FP8X4),
-                scales=w_scales[a][:, cols],
-                in_=w_grp[a][:, cols, :].rearrange("p n t -> p (n t)"),
-            )
-
-        def multiply(acc, i, h, a):
-            tokens = slice(P * i, P * (i + 1))
-            cols = slice(H * h, H * (h + 1))
-            nc.tensor.matmul_mx(
-                out=acc[:, H * (i % 2) : H * (i % 2 + 1)],
-                lhsT=g_words[a][:, tokens].bitcast(FP8X4),
-                lhsT_scale=g_planes[4 * a : P, tokens],
-                rhs=w_codes[a][:, cols].bitcast(FP8X4),
-                rhs_scale=w_scales[a][:, cols],
-                start=(a == 0),
-                stop=(a == PASSES - 1),
-            )
-
-        def finish(acc, pair, h, tiles):
-            for us in tiles:
-                part = slice(H * us[0], H * (us[-1] + 1))
-                width = H * len(us)
-                summed = stage.tile([P, width], F32, name="summed")
-                nc.vector.tensor_tensor(
-                    summed[:], acc[:, part], bias[:, h, us[0] : us[-1] + 1, :].rearrange("p u n -> p (u n)"), ADD
-                )
-                result = stage.tile([P, width], F32, name="result")
-                nc.scalar.activation(result[:], summed[:], GELU)
-                t0 = 2 * P * pair + P * us[0]
-                nc.sync.dma_start(
-                    out=out[t0 : t0 + P * len(us), H * h : H * (h + 1)].rearrange("(u q) n -> q u n", q=P),
-                    in_=result[:].rearrange("p (u n) -> p u n", n=H),
-                )
-
-        for a in range(PASSES):
-            prepare(a, 0, 208)
         gather_words(0, 0, S)
+        nc.vector.tensor_copy(g_planes[:], planes[:].indirect(offsets[:]))
+        quantise(group(raw0[0], nc.scalar.copy, "slot_a"), 0, 0)
+        raw1 = load_w(1, 1, 8192)
+        load_words(2, laid.tile([P, T], I32, align_bytes=64, offset=16384, name="words2"))
         gather_words(1, 0, S)
-        gather_planes()
-        words.append(turns.tile([P, T], I32, align_bytes=64, name="words_even"))
-        load_words(2)
-        for a in range(PASSES):
-            prepare(a, 1, 160)
-        accs = [psum.tile([P, N], F32, name="acc") for pair in range(PAIRS)]
+        quantise(group(raw1[0], nc.scalar.copy, "w_grp1"), 1, 0)
+        raw2 = load_w(2, 2, 4096)
+        accs = [psum.tile([P, N], F32, name="acc") for i in range(BANKS)]
         for a in range(PASSES - 1):
-            for pair in range(PAIRS):
-                multiply(accs[pair], 2 * pair, 0, a)
-        for pair in range(PAIRS):
-            if pair % 2 == 0:
-                gather_words(2, 2 * P * pair, 2 * P * (pair + 2))
-            multiply(accs[pair], 2 * pair, 0, PASSES - 1)
-            for a in range(PASSES):
-                multiply(accs[pair], 2 * pair + 1, 0, a)
-            finish(accs[pair], pair, 0, ((0, 1),))
-        for pair in range(PAIRS):
-            acc = psum.tile([P, N], F32, name="acc")
-            for u in range(2):
+            for i in range(BANKS):
+                multiply(accs[i], i, a)
+        for q in range(4):
+            gather_words(2, 512 * q, 512 * (q + 1))
+        for h in range(2):
+            quantise(group(raw2[h], nc.scalar.copy, f"w_grp2_{h}"), 2, H * h)
+        for i in range(TILES):
+            if i < BANKS:
+                acc = accs[i]
+                multiply(acc, i, PASSES - 1)
+            else:
+                acc = psum.tile([P, N], F32, name="acc")
                 for a in range(PASSES):
-                    multiply(acc, 2 * pair + u, 1, a)
-            finish(acc, pair, 1, ((0, 1),) if pair < PAIRS - 1 else ((0,), (1,)))
+                    multiply(acc, i, a)
+            finish(acc, i, ((0, N),) if i < TILES - 1 else ((0, H), (H, N)))

@@ -34,16 +34,17 @@ def tile_list_tabw_tm_gelu_kernel(tc, tab, w, b, offs, out):
         planes = keep.tile([P, T], U8, align_bytes=64, name="planes")
         w_codes = [keep.tile([P, N], U32, align_bytes=64, name=f"w_codes{a}") for a in range(PASSES)]
         w_scales = [keep.tile([P, N], U8, align_bytes=64, name=f"w_scales{a}") for a in range(PASSES)]
-        g_words = [keep.tile([P, S], U32, align_bytes=64, name=f"g_words{a}") for a in range(PASSES)]
         g_planes = keep.tile([P, S], U8, align_bytes=64, name="g_planes")
         bias = keep.tile([P, N], F32, align_bytes=64, name="bias")
-        b_cols = keep.tile([P, 4], F32, align_bytes=64, name="slot_b")
-        warm = keep.tile([P, 1], F32, align_bytes=64, name="slot_a")
+        warm = keep.tile([P, 1], F32, name="warm")
+        ident = laid.tile([P, P], F32, align_bytes=64, offset=16384 - 256, name="ident")
+        b_cols = laid.tile([P, 4], F32, align_bytes=64, offset=24576, name="b_cols")
         words = {}
+        picked = {}
 
         def load_words(a, tile):
             words[a] = tile
-            nc.sync.dma_start(out=words[a][:], in_=tab[a, 0 : 512 * T].rearrange("(p x) -> p x", p=P).bitcast(I32))
+            nc.sync.dma_start(out=tile[:], in_=tab[a, 0 : 512 * T].rearrange("(p x) -> p x", p=P).bitcast(I32))
 
         def load_w(a, parts, offset):
             width = N // parts
@@ -72,35 +73,38 @@ def tile_list_tabw_tm_gelu_kernel(tc, tab, w, b, offs, out):
                 in_=grouped[:].rearrange("p n t -> p (n t)"),
             )
 
-        def gather_words(a, j0, j1):
-            nc.vector.tensor_copy(g_words[a][:, j0:j1], words[a][:].bitcast(U32).indirect(offsets[:, j0 // 16 : j1 // 16]))
+        def gather_words(a, j0, j1, name):
+            tile = keep.tile([P, j1 - j0], U32, align_bytes=64, name=name)
+            nc.vector.tensor_copy(tile[:], words[a][:].bitcast(U32).indirect(offsets[:, j0 // 16 : j1 // 16]))
+            for i in range(j0 // P, j1 // P):
+                picked[(a, i)] = tile[:, P * i - j0 : P * (i + 1) - j0]
 
         def multiply(acc, i, a):
-            tokens = slice(P * i, P * (i + 1))
             nc.tensor.matmul_mx(
                 out=acc[:],
-                lhsT=g_words[a][:, tokens].bitcast(FP8X4),
-                lhsT_scale=g_planes[4 * a : P, tokens],
+                lhsT=picked[(a, i)].bitcast(FP8X4),
+                lhsT_scale=g_planes[4 * a : P, P * i : P * (i + 1)],
                 rhs=w_codes[a][:].bitcast(FP8X4),
                 rhs_scale=w_scales[a][:],
                 start=(a == 0),
                 stop=(a == PASSES - 1),
             )
 
-        def finish(acc, i, parts):
+        def finish(acc, i, parts, pool, name):
             for n0, n1 in parts:
-                summed = stage.tile([P, n1 - n0], F32, name="summed")
+                summed = pool.tile([P, n1 - n0], F32, align_bytes=64, name=name)
                 nc.vector.tensor_tensor(summed[:], acc[:, n0:n1], bias[:, n0:n1], ADD)
                 result = stage.tile([P, n1 - n0], F32, name="result")
                 nc.scalar.activation(result[:], summed[:], GELU)
                 nc.sync.dma_start(out=out[P * i : P * (i + 1), n0:n1], in_=result[:])
 
         nc.vector.memset(planes[:].bitcast(I32), 0)
-        nc.vector.memset(warm[:], 0.0)
+        nc.gpsimd.memset(warm[:], 0.0)
         nc.sync.dma_start(offsets[:], offs)
         load_words(0, keep.tile([P, T], I32, align_bytes=64, name="words0"))
         nc.sync.dma_start(out=b_cols[:], in_=b.rearrange("(p c) -> p c", c=4))
-        raw0 = load_w(0, 1, 12288)
+        raw0 = load_w(0, 1, 40960)
+        make_identity(nc, ident[:])
         scale_rows = tab[:, 512 * T : 528 * T].rearrange("a (q t) -> a q t", t=T)
         for quad in range(4):
             nc.gpsimd.dma_start(
@@ -108,30 +112,29 @@ def tile_list_tabw_tm_gelu_kernel(tc, tab, w, b, offs, out):
                 in_=scale_rows[:, 4 * quad : 4 * quad + 4, :].bitcast(I32),
             )
         nc.scalar.activation(warm[:], warm[:], GELU)
-        ident = keep.tile([P, P], F32, align_bytes=64, name="slot_a")
-        make_identity(nc, ident[:])
         spread = psum.tile([P, N], F32, name="acc")
         for c in range(4):
             nc.tensor.transpose(spread[:, P * c : P * (c + 1)], b_cols[:, c : c + 1].to_broadcast([P, P]), ident[:])
         nc.scalar.copy(bias[:].rearrange("p (m c) -> p m c", c=4), spread[:].rearrange("p (c m) -> p m c", c=4))
-        load_words(1, keep.tile([P, T], I32, align_bytes=64, name="slot_b"))
+        load_words(1, laid.tile([P, T], I32, align_bytes=64, offset=0, name="words1"))
+        raw1 = load_w(1, 1, 16384)
+        load_words(2, laid.tile([P, T], I32, align_bytes=64, offset=24576, name="words2"))
 
-        gather_words(0, 0, S)
+        gather_words(0, 0, S, "picked0")
         nc.vector.tensor_copy(g_planes[:], planes[:].indirect(offsets[:]))
-        quantise(group(raw0[0], nc.scalar.copy, "slot_a"), 0, 0)
-        raw1 = load_w(1, 1, 8192)
-        load_words(2, laid.tile([P, T], I32, align_bytes=64, offset=16384, name="words2"))
-        gather_words(1, 0, S)
+        quantise(group(raw0[0], nc.scalar.copy, "w_grp0"), 0, 0)
+        raw2 = load_w(2, 2, 45056)
+        gather_words(1, 0, S, "picked1")
         quantise(group(raw1[0], nc.scalar.copy, "w_grp1"), 1, 0)
-        raw2 = load_w(2, 2, 4096)
         accs = [psum.tile([P, N], F32, name="acc") for i in range(BANKS)]
         for a in range(PASSES - 1):
             for i in range(BANKS):
                 multiply(accs[i], i, a)
-        for q in range(4):
-            gather_words(2, 512 * q, 512 * (q + 1))
+        for q in range(2):
+            gather_words(2, 512 * q, 512 * (q + 1), f"picked2_{q}")
         for h in range(2):
             quantise(group(raw2[h], nc.scalar.copy, f"w_grp2_{h}"), 2, H * h)
+        late = {2: 2, 6: 3}
         for i in range(TILES):
             if i < BANKS:
                 acc = accs[i]
@@ -140,4 +143,8 @@ def tile_list_tabw_tm_gelu_kernel(tc, tab, w, b, offs, out):
                 acc = psum.tile([P, N], F32, name="acc")
                 for a in range(PASSES):
                     multiply(acc, i, a)
-            finish(acc, i, ((0, N),) if i < TILES - 1 else ((0, H), (H, N)))
+            if i in late:
+                finish(acc, i, ((0, N),), keep, f"late{i}")
+                gather_words(2, 512 * late[i], 512 * (late[i] + 1), f"late{i}")
+            else:
+                finish(acc, i, ((0, N),) if i < TILES - 1 else ((0, H), (H, N)), stage, "summed")

@@ -27,46 +27,41 @@ def tile_list_tabw_tm_gelu_kernel(tc, tab, w, b, offs, out):
     with ExitStack() as ctx:
         keep = ctx.enter_context(tc.tile_pool(name="keep", bufs=1))
         laid = ctx.enter_context(tc.tile_pool(name="laid", bufs=1))
-        stage = ctx.enter_context(tc.tile_pool(name="stage", bufs=6))
-        psum = ctx.enter_context(tc.psum_pool(name="psum", bufs=BANKS))
+        stage = ctx.enter_context(tc.tile_pool(name="stage", bufs=17))
+        psum = ctx.enter_context(tc.psum_pool(name="psum", bufs=1))
 
         offsets = keep.tile([P, S // 16], U16, name="offsets")
         planes = keep.tile([P, T], U8, align_bytes=64, name="planes")
         w_codes = [keep.tile([P, N], U32, align_bytes=64, name=f"w_codes{a}") for a in range(PASSES)]
         w_scales = [keep.tile([P, N], U8, align_bytes=64, name=f"w_scales{a}") for a in range(PASSES)]
         g_planes = keep.tile([P, S], U8, align_bytes=64, name="g_planes")
-        bias = keep.tile([P, N], F32, align_bytes=64, name="bias")
+        bias = keep.tile([P, 2 * N], F32, align_bytes=64, name="bias")
         warm = keep.tile([P, 1], F32, name="warm")
         ident = laid.tile([P, P], F32, align_bytes=64, offset=16384 - 256, name="ident")
-        b_cols = laid.tile([P, 4], F32, align_bytes=64, offset=24576, name="b_cols")
+        b_rows = laid.tile([P, 4], F32, align_bytes=64, offset=20480, name="b_rows")
         words = {}
         picked = {}
+
+        def bank(k):
+            return psum.tile([P, N], F32, name=f"bank{k}")
 
         def load_words(a, tile):
             words[a] = tile
             nc.sync.dma_start(out=tile[:], in_=tab[a, 0 : 512 * T].rearrange("(p x) -> p x", p=P).bitcast(I32))
 
-        def load_w(a, parts, offset):
-            width = N // parts
-            raw = laid.tile([P, parts, 4, width], F32, align_bytes=64, offset=offset, name=f"w_raw{a}")
-            for h in range(parts):
-                nc.sync.dma_start(
-                    out=raw[:, h],
-                    in_=w[512 * a : 512 * (a + 1), width * h : width * (h + 1)].rearrange("(p j) n -> p j n", j=4),
-                )
-            return [raw[:, h] for h in range(parts)]
+        def load_w(a, n0, n1, offset):
+            raw = laid.tile([P, 4, n1 - n0], F32, align_bytes=64, offset=offset, name=f"w_raw{a}_{n0}")
+            nc.sync.dma_start(out=raw[:], in_=w[512 * a : 512 * (a + 1), n0:n1].rearrange("(p j) n -> p j n", j=4))
+            return raw
 
-        def group(raw, engine_copy, name):
+        def quantise(raw, a, n0):
             width = raw.shape[2]
-            grouped = keep.tile([P, width, 4], BF16, align_bytes=64, name=name)
-            engine_copy(
+            grouped = keep.tile([P, width, 4], BF16, align_bytes=64, name=f"w_grp{a}_{n0}")
+            nc.scalar.copy(
                 grouped[:].rearrange("p (c i) t -> p c t i", i=4),
-                raw.rearrange("p t (c i) -> p c t i", i=4),
+                raw[:].rearrange("p t (c i) -> p c t i", i=4),
             )
-            return grouped
-
-        def quantise(grouped, a, n0):
-            cols = slice(n0, n0 + grouped.shape[1])
+            cols = slice(n0, n0 + width)
             nc.vector.quantize_mx(
                 out=w_codes[a][:, cols].bitcast(FP8X4),
                 scales=w_scales[a][:, cols],
@@ -79,31 +74,48 @@ def tile_list_tabw_tm_gelu_kernel(tc, tab, w, b, offs, out):
             for i in range(j0 // P, j1 // P):
                 picked[(a, i)] = tile[:, P * i - j0 : P * (i + 1) - j0]
 
-        def multiply(acc, i, a):
+        def multiply(acc, i, a, cols, start, stop):
             nc.tensor.matmul_mx(
-                out=acc[:],
+                out=acc,
                 lhsT=picked[(a, i)].bitcast(FP8X4),
                 lhsT_scale=g_planes[4 * a : P, P * i : P * (i + 1)],
-                rhs=w_codes[a][:].bitcast(FP8X4),
-                rhs_scale=w_scales[a][:],
-                start=(a == 0),
-                stop=(a == PASSES - 1),
+                rhs=w_codes[a][:, cols].bitcast(FP8X4),
+                rhs_scale=w_scales[a][:, cols],
+                start=start,
+                stop=stop,
             )
 
-        def finish(acc, i, parts, pool, name):
+        def multiply_pair(acc, pair, h, a):
+            for u in range(2):
+                multiply(acc[:, H * u : H * (u + 1)], 2 * pair + u, a, slice(H * h, H * (h + 1)),
+                         a == 0 and u == 0, a == PASSES - 1 and u == 1)
+
+        def activate(acc, bias_part, pool, name):
+            width = acc.shape[1]
+            summed = pool.tile([P, width], F32, align_bytes=64, name=name)
+            nc.vector.tensor_tensor(summed[:], acc, bias_part, ADD)
+            result = stage.tile([P, width], F32, name="result")
+            nc.scalar.activation(result[:], summed[:], GELU)
+            return result
+
+        def finish_pair(acc, pair, h, pool, name):
+            result = activate(acc[:], bias[:, N * h : N * (h + 1)], pool, name)
+            nc.sync.dma_start(
+                out=out[2 * P * pair : 2 * P * (pair + 1), H * h : H * (h + 1)].rearrange("(u q) n -> q u n", q=P),
+                in_=result[:].rearrange("p (u n) -> p u n", n=H),
+            )
+
+        def finish(acc, i, parts):
             for n0, n1 in parts:
-                summed = pool.tile([P, n1 - n0], F32, align_bytes=64, name=name)
-                nc.vector.tensor_tensor(summed[:], acc[:, n0:n1], bias[:, n0:n1], ADD)
-                result = stage.tile([P, n1 - n0], F32, name="result")
-                nc.scalar.activation(result[:], summed[:], GELU)
+                result = activate(acc[:, n0:n1], bias[:, H + n0 : H + n1], stage, "summed")
                 nc.sync.dma_start(out=out[P * i : P * (i + 1), n0:n1], in_=result[:])
 
         nc.vector.memset(planes[:].bitcast(I32), 0)
         nc.gpsimd.memset(warm[:], 0.0)
         nc.sync.dma_start(offsets[:], offs)
         load_words(0, keep.tile([P, T], I32, align_bytes=64, name="words0"))
-        nc.sync.dma_start(out=b_cols[:], in_=b.rearrange("(p c) -> p c", c=4))
-        raw0 = load_w(0, 1, 40960)
+        nc.sync.dma_start(out=b_rows[:], in_=b.rearrange("(p c) -> p c", c=4))
+        raw0 = load_w(0, 0, N, 40960)
         make_identity(nc, ident[:])
         scale_rows = tab[:, 512 * T : 528 * T].rearrange("a (q t) -> a q t", t=T)
         for quad in range(4):
@@ -112,39 +124,56 @@ def tile_list_tabw_tm_gelu_kernel(tc, tab, w, b, offs, out):
                 in_=scale_rows[:, 4 * quad : 4 * quad + 4, :].bitcast(I32),
             )
         nc.scalar.activation(warm[:], warm[:], GELU)
-        spread = psum.tile([P, N], F32, name="acc")
+        spread = bank(0)
         for c in range(4):
-            nc.tensor.transpose(spread[:, P * c : P * (c + 1)], b_cols[:, c : c + 1].to_broadcast([P, P]), ident[:])
-        nc.scalar.copy(bias[:].rearrange("p (m c) -> p m c", c=4), spread[:].rearrange("p (c m) -> p m c", c=4))
+            nc.tensor.transpose(spread[:, P * c : P * (c + 1)], b_rows[:, c : c + 1].to_broadcast([P, P]), ident[:])
+        for u in range(2):
+            nc.scalar.copy(
+                bias[:].rearrange("p (h u m c) -> p u h m c", h=2, u=2, c=4)[:, u],
+                spread[:].rearrange("p (c h m) -> p h m c", c=4, h=2),
+            )
         load_words(1, laid.tile([P, T], I32, align_bytes=64, offset=0, name="words1"))
-        raw1 = load_w(1, 1, 16384)
-        load_words(2, laid.tile([P, T], I32, align_bytes=64, offset=24576, name="words2"))
+        raw1 = load_w(1, 0, H, 16384)
+        load_words(2, laid.tile([P, T], I32, align_bytes=64, offset=20480, name="words2"))
 
         gather_words(0, 0, S, "picked0")
         nc.vector.tensor_copy(g_planes[:], planes[:].indirect(offsets[:]))
-        quantise(group(raw0[0], nc.scalar.copy, "w_grp0"), 0, 0)
-        raw2 = load_w(2, 2, 45056)
-        gather_words(1, 0, S, "picked1")
-        quantise(group(raw1[0], nc.scalar.copy, "w_grp1"), 1, 0)
-        accs = [psum.tile([P, N], F32, name="acc") for i in range(BANKS)]
-        for a in range(PASSES - 1):
-            for i in range(BANKS):
-                multiply(accs[i], i, a)
+        quantise(raw0, 0, 0)
+        raw2 = load_w(2, 0, H, 36864 + 64)
+        raw1_late = load_w(1, H, N, 36864 + 64 + 4096)
+        raw2_late = load_w(2, H, N, 36864 + 64 + 8192)
+        gather_words(1, 0, 1536, "picked1")
+        quantise(raw1, 1, 0)
+        accs = [bank(k) for k in range(BANKS)]
+        for pair in range(4):
+            multiply_pair(accs[pair], pair, 0, 0)
+        for pair in range(4):
+            multiply_pair(accs[4 + pair], pair, 1, 0)
+        for pair in range(4):
+            multiply_pair(accs[pair], pair, 0, 1)
         for q in range(2):
             gather_words(2, 512 * q, 512 * (q + 1), f"picked2_{q}")
-        for h in range(2):
-            quantise(group(raw2[h], nc.scalar.copy, f"w_grp2_{h}"), 2, H * h)
-        late = {2: 2, 6: 3}
-        for i in range(TILES):
-            if i < BANKS:
-                acc = accs[i]
-                multiply(acc, i, PASSES - 1)
+        quantise(raw2, 2, 0)
+        gather_words(1, 1536, S, "w_grp2_0")
+        for pair in range(4):
+            multiply_pair(accs[pair], pair, 0, 2)
+        quantise(raw1_late, 1, H)
+        for pair in range(4):
+            multiply_pair(accs[4 + pair], pair, 1, 1)
+        late = {1: 2, 5: 3}
+        for k in range(BANKS):
+            pair, h = k % 4, k // 4
+            if k == 2:
+                quantise(raw2_late, 2, H)
+                for other in range(4):
+                    multiply_pair(accs[4 + other], other, 1, 2)
+            if k in late:
+                finish_pair(accs[k], pair, h, keep, f"late{k}")
+                gather_words(2, 512 * late[k], 512 * (late[k] + 1), f"late{k}")
             else:
-                acc = psum.tile([P, N], F32, name="acc")
-                for a in range(PASSES):
-                    multiply(acc, i, a)
-            if i in late:
-                finish(acc, i, ((0, N),), keep, f"late{i}")
-                gather_words(2, 512 * late[i], 512 * (late[i] + 1), f"late{i}")
-            else:
-                finish(acc, i, ((0, N),) if i < TILES - 1 else ((0, H), (H, N)), stage, "summed")
+                finish_pair(accs[k], pair, h, stage, "summed")
+        for i in range(BANKS, TILES):
+            acc = bank(i - BANKS)
+            for a in range(PASSES):
+                multiply(acc[:], i, a, slice(0, N), a == 0, a == PASSES - 1)
+            finish(acc, i, ((0, N),) if i < TILES - 1 else ((0, H), (H, N)))

@@ -27,20 +27,24 @@ def tile_list_tabw_tm_gelu_kernel(tc, tab, w, b, offs, out):
     with ExitStack() as ctx:
         keep = ctx.enter_context(tc.tile_pool(name="keep", bufs=1))
         laid = ctx.enter_context(tc.tile_pool(name="laid", bufs=1))
-        stage = ctx.enter_context(tc.tile_pool(name="stage", bufs=17))
+        stage = ctx.enter_context(tc.tile_pool(name="stage", bufs=13))
         psum = ctx.enter_context(tc.psum_pool(name="psum", bufs=1))
 
         offsets = keep.tile([P, S // 16], U16, name="offsets")
-        planes = keep.tile([P, T], U8, align_bytes=64, name="planes")
-        w_codes = [keep.tile([P, N], U32, align_bytes=64, name=f"w_codes{a}") for a in range(PASSES)]
+        planes = laid.tile([P, T], U8, align_bytes=64, offset=49152, name="planes")
+        w_codes = [laid.tile([P, N], U32, align_bytes=64, offset=49152, name="w_codes0")]
+        w_codes.extend(keep.tile([P, N], U32, align_bytes=64, name=f"w_codes{a}") for a in range(1, PASSES))
         w_scales = [keep.tile([P, N], U8, align_bytes=64, name=f"w_scales{a}") for a in range(PASSES)]
         g_planes = keep.tile([P, S], U8, align_bytes=64, name="g_planes")
-        bias = keep.tile([P, 2 * N], F32, align_bytes=64, name="bias")
+        bias = keep.tile([P, N + H], F32, align_bytes=64, name="bias")
+        bias_col = keep.tile([P, 2], F32, align_bytes=64, name="bias_col")
         warm = keep.tile([P, 1], F32, name="warm")
-        ident = laid.tile([P, P], F32, align_bytes=64, offset=16384 - 256, name="ident")
-        b_rows = laid.tile([P, 4], F32, align_bytes=64, offset=20480, name="b_rows")
+        ident = keep.tile([P, P], F32, align_bytes=64, name="ident")
+        b_rows = laid.tile([P, 4], F32, align_bytes=64, offset=0, name="b_rows")
         words = {}
         picked = {}
+        runs = {}
+        late_codes = []
 
         def bank(k):
             return psum.tile([P, N], F32, name=f"bank{k}")
@@ -52,24 +56,39 @@ def tile_list_tabw_tm_gelu_kernel(tc, tab, w, b, offs, out):
         def load_w(a, n0, n1, offset):
             raw = laid.tile([P, 4, n1 - n0], F32, align_bytes=64, offset=offset, name=f"w_raw{a}_{n0}")
             nc.sync.dma_start(out=raw[:], in_=w[512 * a : 512 * (a + 1), n0:n1].rearrange("(p j) n -> p j n", j=4))
-            return raw
+            return raw[:]
 
-        def quantise(raw, a, n0):
+        def load_halves(a, offset):
+            raw = laid.tile([P, 2, 4, H], F32, align_bytes=64, offset=offset, name=f"w_raw{a}")
+            for h in range(2):
+                nc.sync.dma_start(
+                    out=raw[:, h],
+                    in_=w[512 * a : 512 * (a + 1), H * h : H * (h + 1)].rearrange("(p j) n -> p j n", j=4),
+                )
+            return raw[:, 0], raw[:, 1]
+
+        def codes(a, cols):
+            if a == PASSES - 1 and cols.start >= H:
+                return late_codes[0][:, cols.start - H : cols.stop - H]
+            return w_codes[a][:, cols]
+
+        def quantise(raw, a, n0, offset):
             width = raw.shape[2]
-            grouped = keep.tile([P, width, 4], BF16, align_bytes=64, name=f"w_grp{a}_{n0}")
+            grouped = laid.tile([P, width, 4], BF16, align_bytes=64, offset=offset, name=f"w_grp{a}_{n0}")
             nc.scalar.copy(
                 grouped[:].rearrange("p (c i) t -> p c t i", i=4),
-                raw[:].rearrange("p t (c i) -> p c t i", i=4),
+                raw.rearrange("p t (c i) -> p c t i", i=4),
             )
             cols = slice(n0, n0 + width)
             nc.vector.quantize_mx(
-                out=w_codes[a][:, cols].bitcast(FP8X4),
+                out=codes(a, cols).bitcast(FP8X4),
                 scales=w_scales[a][:, cols],
                 in_=grouped[:].rearrange("p n t -> p (n t)"),
             )
 
-        def gather_words(a, j0, j1, name):
-            tile = keep.tile([P, j1 - j0], U32, align_bytes=64, name=name)
+        def gather_words(a, j0, j1, offset):
+            tile = laid.tile([P, j1 - j0], U32, align_bytes=64, offset=offset, name=f"picked{a}_{j0}")
+            runs[(a, j0)] = tile
             nc.vector.tensor_copy(tile[:], words[a][:].bitcast(U32).indirect(offsets[:, j0 // 16 : j1 // 16]))
             for i in range(j0 // P, j1 // P):
                 picked[(a, i)] = tile[:, P * i - j0 : P * (i + 1) - j0]
@@ -79,7 +98,7 @@ def tile_list_tabw_tm_gelu_kernel(tc, tab, w, b, offs, out):
                 out=acc,
                 lhsT=picked[(a, i)].bitcast(FP8X4),
                 lhsT_scale=g_planes[4 * a : P, P * i : P * (i + 1)],
-                rhs=w_codes[a][:, cols].bitcast(FP8X4),
+                rhs=codes(a, cols).bitcast(FP8X4),
                 rhs_scale=w_scales[a][:, cols],
                 start=start,
                 stop=stop,
@@ -90,16 +109,44 @@ def tile_list_tabw_tm_gelu_kernel(tc, tab, w, b, offs, out):
                 multiply(acc[:, H * u : H * (u + 1)], 2 * pair + u, a, slice(H * h, H * (h + 1)),
                          a == 0 and u == 0, a == PASSES - 1 and u == 1)
 
-        def activate(acc, bias_part, pool, name):
-            width = acc.shape[1]
-            summed = pool.tile([P, width], F32, align_bytes=64, name=name)
+        def multiply_turned(acc, j0, c, a, run):
+            nc.tensor.matmul_mx(
+                out=acc[:],
+                lhsT=w_codes[a][:, P * c : P * (c + 1)].bitcast(FP8X4),
+                lhsT_scale=w_scales[a][:, P * c : P * (c + 1)],
+                rhs=run.bitcast(FP8X4),
+                rhs_scale=g_planes[4 * a : P, j0 : j0 + N],
+                start=(a == 0),
+                stop=(a == PASSES - 1),
+            )
+
+        def activate_turned(k):
+            active = laid.tile([P, N], F32, align_bytes=64, offset=90112 + 6144 * k + 1984, name=f"active{k}")
+            nc.scalar.activation(active[:], accs[k][:], GELU, bias=bias_col[:, k % 2 : k % 2 + 1])
+            return active
+
+        def finish_turned(chunk):
+            result = keep.tile([P, 4, H], F32, align_bytes=64, name=f"turned{chunk}")
+            for c in range(2):
+                k = 2 * chunk + c
+                back = bank(k)
+                for u in range(4):
+                    nc.tensor.transpose(back[:, P * u : P * (u + 1)], actives[k][:, P * u : P * (u + 1)], ident[:])
+                nc.scalar.copy(result[:, :, P * c : P * (c + 1)], back[:].rearrange("p (u m) -> p u m", m=P))
+            nc.sync.dma_start(
+                out=out[N * chunk : N * (chunk + 1), 0:H].rearrange("(u q) n -> q u n", q=P), in_=result[:]
+            )
+
+        def activate(acc, bias_part, result):
+            summed = stage.tile([P, acc.shape[1]], F32, align_bytes=64, name="summed")
             nc.vector.tensor_tensor(summed[:], acc, bias_part, ADD)
-            result = stage.tile([P, width], F32, name="result")
             nc.scalar.activation(result[:], summed[:], GELU)
             return result
 
-        def finish_pair(acc, pair, h, pool, name):
-            result = activate(acc[:], bias[:, N * h : N * (h + 1)], pool, name)
+        def finish_pair(acc, pair, h):
+            offset = 90112 + 6144 * (3 - pair // 2) + 3968 * (pair % 2)
+            result = laid.tile([P, N], F32, align_bytes=64, offset=offset, name=f"result{pair}")
+            activate(acc[:], bias[:, H : H + N], result)
             nc.sync.dma_start(
                 out=out[2 * P * pair : 2 * P * (pair + 1), H * h : H * (h + 1)].rearrange("(u q) n -> q u n", q=P),
                 in_=result[:].rearrange("p (u n) -> p u n", n=H),
@@ -107,7 +154,7 @@ def tile_list_tabw_tm_gelu_kernel(tc, tab, w, b, offs, out):
 
         def finish(acc, i, parts):
             for n0, n1 in parts:
-                result = activate(acc[:, n0:n1], bias[:, H + n0 : H + n1], stage, "summed")
+                result = activate(acc[:, n0:n1], bias[:, n0:n1], stage.tile([P, n1 - n0], F32, name="result"))
                 nc.sync.dma_start(out=out[P * i : P * (i + 1), n0:n1], in_=result[:])
 
         nc.vector.memset(planes[:].bitcast(I32), 0)
@@ -115,7 +162,7 @@ def tile_list_tabw_tm_gelu_kernel(tc, tab, w, b, offs, out):
         nc.sync.dma_start(offsets[:], offs)
         load_words(0, keep.tile([P, T], I32, align_bytes=64, name="words0"))
         nc.sync.dma_start(out=b_rows[:], in_=b.rearrange("(p c) -> p c", c=4))
-        raw0 = load_w(0, 0, N, 40960)
+        raw0 = load_w(0, 0, N, 28672)
         make_identity(nc, ident[:])
         scale_rows = tab[:, 512 * T : 528 * T].rearrange("a (q t) -> a q t", t=T)
         for quad in range(4):
@@ -127,53 +174,57 @@ def tile_list_tabw_tm_gelu_kernel(tc, tab, w, b, offs, out):
         spread = bank(0)
         for c in range(4):
             nc.tensor.transpose(spread[:, P * c : P * (c + 1)], b_rows[:, c : c + 1].to_broadcast([P, P]), ident[:])
-        for u in range(2):
-            nc.scalar.copy(
-                bias[:].rearrange("p (h u m c) -> p u h m c", h=2, u=2, c=4)[:, u],
-                spread[:].rearrange("p (c h m) -> p h m c", c=4, h=2),
-            )
+        nc.scalar.copy(bias[:, 0:N].rearrange("p (m c) -> p m c", c=4), spread[:].rearrange("p (c m) -> p m c", c=4))
+        nc.scalar.copy(
+            bias[:, N : N + H].rearrange("p (m c) -> p m c", c=4),
+            spread[:].rearrange("p (c m) -> p m c", c=4)[:, P // 2 : P, :],
+        )
+        upright = bank(1)
+        for c in range(2):
+            nc.tensor.transpose(upright[:, P * c : P * (c + 1)], bias[:, P * c : P * (c + 1)], ident[:])
+        nc.scalar.copy(bias_col[:], upright[:, 0:H:P])
         load_words(1, laid.tile([P, T], I32, align_bytes=64, offset=0, name="words1"))
-        raw1 = load_w(1, 0, H, 16384)
-        load_words(2, laid.tile([P, T], I32, align_bytes=64, offset=20480, name="words2"))
 
-        gather_words(0, 0, S, "picked0")
+        gather_words(0, 0, S, 73728)
         nc.vector.tensor_copy(g_planes[:], planes[:].indirect(offsets[:]))
-        quantise(raw0, 0, 0)
-        raw2 = load_w(2, 0, H, 36864 + 64)
-        raw1_late = load_w(1, H, N, 36864 + 64 + 4096)
-        raw2_late = load_w(2, H, N, 36864 + 64 + 8192)
-        gather_words(1, 0, 1536, "picked1")
-        quantise(raw1, 1, 0)
+        quantise(raw0, 0, 0, 57344)
+        raw1 = load_w(1, 0, N, 32768)
+        load_words(2, laid.tile([P, T], I32, align_bytes=64, offset=16384, name="words2"))
+        raw2, raw2_late = load_halves(2, 40896)
+        gather_words(1, 0, S // 2, 51200)
+        quantise(raw1, 1, 0, 86016)
         accs = [bank(k) for k in range(BANKS)]
-        for pair in range(4):
-            multiply_pair(accs[pair], pair, 0, 0)
+        for k in range(4):
+            multiply_turned(accs[k], N * (k // 2), k % 2, 0, runs[(0, 0)][:, N * (k // 2) : N * (k // 2 + 1)])
         for pair in range(4):
             multiply_pair(accs[4 + pair], pair, 1, 0)
-        for pair in range(4):
-            multiply_pair(accs[pair], pair, 0, 1)
-        for q in range(2):
-            gather_words(2, 512 * q, 512 * (q + 1), f"picked2_{q}")
-        quantise(raw2, 2, 0)
-        gather_words(1, 1536, S, "w_grp2_0")
-        for pair in range(4):
-            multiply_pair(accs[pair], pair, 0, 2)
-        quantise(raw1_late, 1, H)
+        for k in range(4):
+            multiply_turned(accs[k], N * (k // 2), k % 2, 1, runs[(1, 0)][:, N * (k // 2) : N * (k // 2 + 1)])
         for pair in range(4):
             multiply_pair(accs[4 + pair], pair, 1, 1)
-        late = {1: 2, 5: 3}
-        for k in range(BANKS):
-            pair, h = k % 4, k // 4
-            if k == 2:
-                quantise(raw2_late, 2, H)
-                for other in range(4):
-                    multiply_pair(accs[4 + other], other, 1, 2)
-            if k in late:
-                finish_pair(accs[k], pair, h, keep, f"late{k}")
-                gather_words(2, 512 * late[k], 512 * (late[k] + 1), f"late{k}")
-            else:
-                finish_pair(accs[k], pair, h, stage, "summed")
+        for q in range(2):
+            gather_words(2, 512 * q, 512 * (q + 1), 81920 + 2048 * q)
+        quantise(raw2, 2, 0, 63488)
+        gather_words(1, 1024, 1536, 63488 + 64)
+        for k in range(4):
+            multiply_turned(accs[k], N * (k // 2), k % 2, 2, runs[(2, N * (k // 2))][:])
+        gather_words(2, 1024, 1536, 63488 + 64 - 2048)
+        actives = [activate_turned(k) for k in range(2)]
+        finish_turned(0)
+        late_codes.append(laid.tile([P, H], U32, align_bytes=64, offset=90112 + 6144 + 1984, name="late_codes"))
+        quantise(raw2_late, 2, H, 67712)
+        gather_words(1, 1536, S, 67712 + 64 - 2048)
+        gather_words(2, 1536, S, 67712 + 64)
+        actives.extend(activate_turned(k) for k in range(2, 4))
+        finish_turned(1)
+        for pair in range(4):
+            multiply_pair(accs[4 + pair], pair, 1, 2)
+        for pair in range(4):
+            finish_pair(accs[4 + pair], pair, 1)
         for i in range(BANKS, TILES):
             acc = bank(i - BANKS)
-            for a in range(PASSES):
-                multiply(acc[:], i, a, slice(0, N), a == 0, a == PASSES - 1)
+            for a in range(PASSES - 1):
+                multiply(acc[:], i, a, slice(0, N), a == 0, False)
+            for h in range(2):
+                multiply(acc[:, H * h : H * (h + 1)], i, PASSES - 1, slice(H * h, H * (h + 1)), False, h == 1)
             finish(acc, i, ((0, N),) if i < TILES - 1 else ((0, H), (H, N)))

@@ -27,24 +27,21 @@ def tile_list_tabw_tm_gelu_kernel(tc, tab, w, b, offs, out):
     with ExitStack() as ctx:
         keep = ctx.enter_context(tc.tile_pool(name="keep", bufs=1))
         laid = ctx.enter_context(tc.tile_pool(name="laid", bufs=1))
-        stage = ctx.enter_context(tc.tile_pool(name="stage", bufs=13))
         psum = ctx.enter_context(tc.psum_pool(name="psum", bufs=1))
 
         offsets = keep.tile([P, S // 16], U16, name="offsets")
-        planes = laid.tile([P, T], U8, align_bytes=64, offset=49152, name="planes")
-        w_codes = [laid.tile([P, N], U32, align_bytes=64, offset=49152, name="w_codes0")]
+        planes = laid.tile([P, T], U8, align_bytes=64, offset=59328, name="planes")
+        w_codes = [laid.tile([P, N], U32, align_bytes=64, offset=57344, name="w_codes0")]
         w_codes.extend(keep.tile([P, N], U32, align_bytes=64, name=f"w_codes{a}") for a in range(1, PASSES))
         w_scales = [keep.tile([P, N], U8, align_bytes=64, name=f"w_scales{a}") for a in range(PASSES)]
         g_planes = keep.tile([P, S], U8, align_bytes=64, name="g_planes")
-        bias = keep.tile([P, N + H], F32, align_bytes=64, name="bias")
-        bias_col = keep.tile([P, 2], F32, align_bytes=64, name="bias_col")
+        bias = keep.tile([P, N], F32, align_bytes=64, name="bias")
+        bias_col = keep.tile([P, 4], F32, align_bytes=64, name="bias_col")
         warm = keep.tile([P, 1], F32, name="warm")
         ident = keep.tile([P, P], F32, align_bytes=64, name="ident")
-        b_rows = laid.tile([P, 4], F32, align_bytes=64, offset=0, name="b_rows")
+        b_rows = laid.tile([P, 32], F32, align_bytes=64, offset=16384 - 64, name="b_rows")
         words = {}
-        picked = {}
         runs = {}
-        late_codes = []
 
         def bank(k):
             return psum.tile([P, N], F32, name=f"bank{k}")
@@ -53,116 +50,89 @@ def tile_list_tabw_tm_gelu_kernel(tc, tab, w, b, offs, out):
             words[a] = tile
             nc.sync.dma_start(out=tile[:], in_=tab[a, 0 : 512 * T].rearrange("(p x) -> p x", p=P).bitcast(I32))
 
-        def load_w(a, n0, n1, offset):
-            raw = laid.tile([P, 4, n1 - n0], F32, align_bytes=64, offset=offset, name=f"w_raw{a}_{n0}")
-            nc.sync.dma_start(out=raw[:], in_=w[512 * a : 512 * (a + 1), n0:n1].rearrange("(p j) n -> p j n", j=4))
-            return raw[:]
+        def load_w(a, offset):
+            raw = laid.tile([P, 4, N], F32, align_bytes=64, offset=offset, name=f"w_raw{a}")
+            nc.sync.dma_start(out=raw[:], in_=w[512 * a : 512 * (a + 1), :].rearrange("(p j) n -> p j n", j=4))
+            return raw
 
-        def load_halves(a, offset):
-            raw = laid.tile([P, 2, 4, H], F32, align_bytes=64, offset=offset, name=f"w_raw{a}")
-            for h in range(2):
-                nc.sync.dma_start(
-                    out=raw[:, h],
-                    in_=w[512 * a : 512 * (a + 1), H * h : H * (h + 1)].rearrange("(p j) n -> p j n", j=4),
-                )
-            return raw[:, 0], raw[:, 1]
-
-        def codes(a, cols):
-            if a == PASSES - 1 and cols.start >= H:
-                return late_codes[0][:, cols.start - H : cols.stop - H]
-            return w_codes[a][:, cols]
-
-        def quantise(raw, a, n0, offset):
-            width = raw.shape[2]
-            grouped = laid.tile([P, width, 4], BF16, align_bytes=64, offset=offset, name=f"w_grp{a}_{n0}")
+        def quantise(raw, a, offset):
+            grouped = laid.tile([P, N, 4], BF16, align_bytes=64, offset=offset, name=f"w_grp{a}")
             nc.scalar.copy(
                 grouped[:].rearrange("p (c i) t -> p c t i", i=4),
-                raw.rearrange("p t (c i) -> p c t i", i=4),
+                raw[:].rearrange("p t (c i) -> p c t i", i=4),
             )
-            cols = slice(n0, n0 + width)
             nc.vector.quantize_mx(
-                out=codes(a, cols).bitcast(FP8X4),
-                scales=w_scales[a][:, cols],
+                out=w_codes[a][:].bitcast(FP8X4),
+                scales=w_scales[a][:],
                 in_=grouped[:].rearrange("p n t -> p (n t)"),
             )
 
         def gather_words(a, j0, j1, offset):
             tile = laid.tile([P, j1 - j0], U32, align_bytes=64, offset=offset, name=f"picked{a}_{j0}")
-            runs[(a, j0)] = tile
             nc.vector.tensor_copy(tile[:], words[a][:].bitcast(U32).indirect(offsets[:, j0 // 16 : j1 // 16]))
             for i in range(j0 // P, j1 // P):
-                picked[(a, i)] = tile[:, P * i - j0 : P * (i + 1) - j0]
+                runs[(a, i)] = (tile, j0)
 
-        def multiply(acc, i, a, cols, start, stop):
-            nc.tensor.matmul_mx(
-                out=acc,
-                lhsT=picked[(a, i)].bitcast(FP8X4),
-                lhsT_scale=g_planes[4 * a : P, P * i : P * (i + 1)],
-                rhs=codes(a, cols).bitcast(FP8X4),
-                rhs_scale=w_scales[a][:, cols],
-                start=start,
-                stop=stop,
-            )
+        def picked(a, j0, j1):
+            tile, first = runs[(a, j0 // P)]
+            return tile[:, j0 - first : j1 - first].bitcast(FP8X4)
 
-        def multiply_pair(acc, pair, h, a):
-            for u in range(2):
-                multiply(acc[:, H * u : H * (u + 1)], 2 * pair + u, a, slice(H * h, H * (h + 1)),
-                         a == 0 and u == 0, a == PASSES - 1 and u == 1)
-
-        def multiply_turned(acc, j0, c, a, run):
+        def multiply(acc, i, a):
             nc.tensor.matmul_mx(
                 out=acc[:],
-                lhsT=w_codes[a][:, P * c : P * (c + 1)].bitcast(FP8X4),
-                lhsT_scale=w_scales[a][:, P * c : P * (c + 1)],
-                rhs=run.bitcast(FP8X4),
-                rhs_scale=g_planes[4 * a : P, j0 : j0 + N],
+                lhsT=picked(a, P * i, P * (i + 1)),
+                lhsT_scale=g_planes[4 * a : P, P * i : P * (i + 1)],
+                rhs=w_codes[a][:].bitcast(FP8X4),
+                rhs_scale=w_scales[a][:],
                 start=(a == 0),
                 stop=(a == PASSES - 1),
             )
 
-        def activate_turned(k):
-            active = laid.tile([P, N], F32, align_bytes=64, offset=90112 + 6144 * k + 1984, name=f"active{k}")
-            nc.scalar.activation(active[:], accs[k][:], GELU, bias=bias_col[:, k % 2 : k % 2 + 1])
+        def multiply_turned(accs, i, a):
+            for c in range(4):
+                nc.tensor.matmul_mx(
+                    out=accs[c // 2][:, H * (c % 2) : H * (c % 2 + 1)],
+                    lhsT=w_codes[a][:, P * c : P * (c + 1)].bitcast(FP8X4),
+                    lhsT_scale=w_scales[a][:, P * c : P * (c + 1)],
+                    rhs=picked(a, P * i, P * i + H),
+                    rhs_scale=g_planes[4 * a : P, P * i : P * i + H],
+                    start=(a == 0 and c % 2 == 0),
+                    stop=(a == PASSES - 1 and c % 2 == 1),
+                )
+
+        def activate_turned(accs, i):
+            active = keep.tile([P, 4, H], F32, align_bytes=64, name=f"active{i}")
+            for c in range(4):
+                nc.scalar.activation(
+                    active[:, c], accs[c // 2][:, H * (c % 2) : H * (c % 2 + 1)], GELU, bias=bias_col[:, c : c + 1]
+                )
             return active
 
-        def finish_turned(chunk):
-            result = keep.tile([P, 4, H], F32, align_bytes=64, name=f"turned{chunk}")
-            for c in range(2):
-                k = 2 * chunk + c
-                back = bank(k)
-                for u in range(4):
-                    nc.tensor.transpose(back[:, P * u : P * (u + 1)], actives[k][:, P * u : P * (u + 1)], ident[:])
-                nc.scalar.copy(result[:, :, P * c : P * (c + 1)], back[:].rearrange("p (u m) -> p u m", m=P))
-            nc.sync.dma_start(
-                out=out[N * chunk : N * (chunk + 1), 0:H].rearrange("(u q) n -> q u n", q=P), in_=result[:]
-            )
+        def turn_back(active, u, k):
+            back = bank(k)
+            for c in range(4):
+                nc.tensor.transpose(back[:, P * c : P * (c + 1)], active[:, c, P * u : P * (u + 1)], ident[:])
+            return back
 
-        def activate(acc, bias_part, result):
-            summed = stage.tile([P, acc.shape[1]], F32, align_bytes=64, name="summed")
-            nc.vector.tensor_tensor(summed[:], acc, bias_part, ADD)
-            nc.scalar.activation(result[:], summed[:], GELU)
-            return result
+        def copy_out(back, i):
+            result = keep.tile([P, N], F32, align_bytes=64, name=f"result{i}")
+            nc.scalar.copy(result[:], back[:])
+            nc.sync.dma_start(out=out[P * i : P * (i + 1), :], in_=result[:])
 
-        def finish_pair(acc, pair, h):
-            offset = 90112 + 6144 * (3 - pair // 2) + 3968 * (pair % 2)
-            result = laid.tile([P, N], F32, align_bytes=64, offset=offset, name=f"result{pair}")
-            activate(acc[:], bias[:, H : H + N], result)
-            nc.sync.dma_start(
-                out=out[2 * P * pair : 2 * P * (pair + 1), H * h : H * (h + 1)].rearrange("(u q) n -> q u n", q=P),
-                in_=result[:].rearrange("p (u n) -> p u n", n=H),
-            )
-
-        def finish(acc, i, parts):
+        def finish(acc, i, parts=((0, N),)):
             for n0, n1 in parts:
-                result = activate(acc[:, n0:n1], bias[:, n0:n1], stage.tile([P, n1 - n0], F32, name="result"))
+                summed = laid.tile([P, n1 - n0], F32, align_bytes=64, offset=90112 + 2048 * i + 4 * n0, name=f"summed{i}_{n0}")
+                result = keep.tile([P, n1 - n0], F32, align_bytes=64, name=f"result{i}_{n0}")
+                nc.vector.tensor_tensor(summed[:], acc[:, n0:n1], bias[:, n0:n1], ADD)
+                nc.scalar.activation(result[:], summed[:], GELU)
                 nc.sync.dma_start(out=out[P * i : P * (i + 1), n0:n1], in_=result[:])
 
         nc.vector.memset(planes[:].bitcast(I32), 0)
         nc.gpsimd.memset(warm[:], 0.0)
         nc.sync.dma_start(offsets[:], offs)
         load_words(0, keep.tile([P, T], I32, align_bytes=64, name="words0"))
-        nc.sync.dma_start(out=b_rows[:], in_=b.rearrange("(p c) -> p c", c=4))
-        raw0 = load_w(0, 0, N, 28672)
+        nc.sync.dma_start(out=b_rows[:, 0:4], in_=b.rearrange("(p c) -> p c", c=4))
+        raw0 = load_w(0, 40896)
         make_identity(nc, ident[:])
         scale_rows = tab[:, 512 * T : 528 * T].rearrange("a (q t) -> a q t", t=T)
         for quad in range(4):
@@ -174,57 +144,49 @@ def tile_list_tabw_tm_gelu_kernel(tc, tab, w, b, offs, out):
         spread = bank(0)
         for c in range(4):
             nc.tensor.transpose(spread[:, P * c : P * (c + 1)], b_rows[:, c : c + 1].to_broadcast([P, P]), ident[:])
-        nc.scalar.copy(bias[:, 0:N].rearrange("p (m c) -> p m c", c=4), spread[:].rearrange("p (c m) -> p m c", c=4))
-        nc.scalar.copy(
-            bias[:, N : N + H].rearrange("p (m c) -> p m c", c=4),
-            spread[:].rearrange("p (c m) -> p m c", c=4)[:, P // 2 : P, :],
-        )
+        nc.scalar.copy(bias[:].rearrange("p (m c) -> p m c", c=4), spread[:].rearrange("p (c m) -> p m c", c=4))
         upright = bank(1)
-        for c in range(2):
+        for c in range(4):
             nc.tensor.transpose(upright[:, P * c : P * (c + 1)], bias[:, P * c : P * (c + 1)], ident[:])
-        nc.scalar.copy(bias_col[:], upright[:, 0:H:P])
+        nc.scalar.copy(bias_col[:], upright[:, 0:N:P])
         load_words(1, laid.tile([P, T], I32, align_bytes=64, offset=0, name="words1"))
+        raw1 = load_w(1, 16384)
 
         gather_words(0, 0, S, 73728)
         nc.vector.tensor_copy(g_planes[:], planes[:].indirect(offsets[:]))
-        quantise(raw0, 0, 0, 57344)
-        raw1 = load_w(1, 0, N, 32768)
-        load_words(2, laid.tile([P, T], I32, align_bytes=64, offset=16384, name="words2"))
-        raw2, raw2_late = load_halves(2, 40896)
-        gather_words(1, 0, S // 2, 51200)
-        quantise(raw1, 1, 0, 86016)
+        quantise(raw0, 0, 63488)
+        raw2 = load_w(2, 49024)
+        load_words(2, laid.tile([P, T], I32, align_bytes=64, offset=24576, name="words2"))
+        gather_words(1, 0, 512, 59392)
+        gather_words(1, 1024, 1536, 61440)
+        quantise(raw1, 1, 86016)
+        gather_words(1, 1536, S, 86016)
+        gather_words(1, 512, 1024, 88064)
+        quantise(raw2, 2, 67584)
         accs = [bank(k) for k in range(BANKS)]
-        for k in range(4):
-            multiply_turned(accs[k], N * (k // 2), k % 2, 0, runs[(0, 0)][:, N * (k // 2) : N * (k // 2 + 1)])
-        for pair in range(4):
-            multiply_pair(accs[4 + pair], pair, 1, 0)
-        for k in range(4):
-            multiply_turned(accs[k], N * (k // 2), k % 2, 1, runs[(1, 0)][:, N * (k // 2) : N * (k // 2 + 1)])
-        for pair in range(4):
-            multiply_pair(accs[4 + pair], pair, 1, 1)
-        for q in range(2):
-            gather_words(2, 512 * q, 512 * (q + 1), 81920 + 2048 * q)
-        quantise(raw2, 2, 0, 63488)
-        gather_words(1, 1024, 1536, 63488 + 64)
-        for k in range(4):
-            multiply_turned(accs[k], N * (k // 2), k % 2, 2, runs[(2, N * (k // 2))][:])
-        gather_words(2, 1024, 1536, 63488 + 64 - 2048)
-        actives = [activate_turned(k) for k in range(2)]
-        finish_turned(0)
-        late_codes.append(laid.tile([P, H], U32, align_bytes=64, offset=90112 + 6144 + 1984, name="late_codes"))
-        quantise(raw2_late, 2, H, 67712)
-        gather_words(1, 1536, S, 67712 + 64 - 2048)
-        gather_words(2, 1536, S, 67712 + 64)
-        actives.extend(activate_turned(k) for k in range(2, 4))
-        finish_turned(1)
-        for pair in range(4):
-            multiply_pair(accs[4 + pair], pair, 1, 2)
-        for pair in range(4):
-            finish_pair(accs[4 + pair], pair, 1)
-        for i in range(BANKS, TILES):
-            acc = bank(i - BANKS)
-            for a in range(PASSES - 1):
-                multiply(acc[:], i, a, slice(0, N), a == 0, False)
-            for h in range(2):
-                multiply(acc[:, H * h : H * (h + 1)], i, PASSES - 1, slice(H * h, H * (h + 1)), False, h == 1)
-            finish(acc, i, ((0, N),) if i < TILES - 1 else ((0, H), (H, N)))
+        for a in range(PASSES):
+            if a == PASSES - 1:
+                gather_words(2, 0, 512, 81920)
+                gather_words(2, 512, 1024, 83968)
+            multiply_turned(accs, 0, a)
+            for i in range(2, BANKS):
+                multiply(accs[i], i, a)
+        active = activate_turned(accs, 0)
+        finish(accs[2], 2)
+        finish(accs[3], 3)
+        for u in range(2):
+            copy_out(turn_back(active, u, u), u)
+        finish(accs[4], 4)
+        finish(accs[5], 5)
+        gather_words(2, 1024, 1536, 90112 + 2048 * 2)
+        finish(accs[6], 6)
+        finish(accs[7], 7)
+        gather_words(2, 1536, S, 90112 + 2048 * 5)
+        for first, banks in ((8, (2, 3, 4, 5)), (12, (0, 1, 6, 7))):
+            late = [bank(k) for k in banks]
+            for u in range(4):
+                for a in range(PASSES - 1):
+                    multiply(late[u], first + u, a)
+            for u in range(4):
+                multiply(late[u], first + u, PASSES - 1)
+                finish(late[u], first + u, ((0, N),) if first + u < TILES - 1 else ((0, H), (H, N)))

@@ -32,14 +32,15 @@ def tile_list_tabw_tm_gelu_kernel(tc, tab, w, b, offs, out):
         offsets = keep.tile([P, S // 16], U16, name="offsets")
         planes = laid.tile([P, T], U8, align_bytes=64, offset=59328, name="planes")
         w_codes = [laid.tile([P, N], U32, align_bytes=64, offset=57344, name="w_codes0")]
-        w_codes.extend(keep.tile([P, N], U32, align_bytes=64, name=f"w_codes{a}") for a in range(1, PASSES))
+        w_codes.append(laid.tile([P, N], U32, align_bytes=64, offset=59392, name="w_codes1"))
+        w_codes.append(keep.tile([P, N], U32, align_bytes=64, name="w_codes2"))
         w_scales = [keep.tile([P, N], U8, align_bytes=64, name=f"w_scales{a}") for a in range(PASSES)]
         g_planes = keep.tile([P, S], U8, align_bytes=64, name="g_planes")
         bias = keep.tile([P, N], F32, align_bytes=64, name="bias")
         bias_col = keep.tile([P, 4], F32, align_bytes=64, name="bias_col")
         warm = keep.tile([P, 1], F32, name="warm")
         ident = keep.tile([P, P], F32, align_bytes=64, name="ident")
-        b_rows = laid.tile([P, 32], F32, align_bytes=64, offset=16384 - 64, name="b_rows")
+        b_rows = laid.tile([P, 4], F32, align_bytes=64, offset=0, name="b_rows")
         words = {}
         runs = {}
 
@@ -77,35 +78,38 @@ def tile_list_tabw_tm_gelu_kernel(tc, tab, w, b, offs, out):
             tile, first = runs[(a, j0 // P)]
             return tile[:, j0 - first : j1 - first].bitcast(FP8X4)
 
-        def multiply(acc, i, a):
+        def multiply(acc, i, a, cols=slice(0, N)):
             nc.tensor.matmul_mx(
-                out=acc[:],
+                out=acc[:, cols],
                 lhsT=picked(a, P * i, P * (i + 1)),
                 lhsT_scale=g_planes[4 * a : P, P * i : P * (i + 1)],
-                rhs=w_codes[a][:].bitcast(FP8X4),
-                rhs_scale=w_scales[a][:],
+                rhs=w_codes[a][:, cols].bitcast(FP8X4),
+                rhs_scale=w_scales[a][:, cols],
                 start=(a == 0),
                 stop=(a == PASSES - 1),
             )
 
+        def chunk_of(accs, c):
+            width = P * len(accs)
+            first = width * c % N
+            return accs[width * c // N][:, first : first + width]
+
         def multiply_turned(accs, i, a):
+            width = P * len(accs)
             for c in range(4):
                 nc.tensor.matmul_mx(
-                    out=accs[c // 2][:, H * (c % 2) : H * (c % 2 + 1)],
+                    out=chunk_of(accs, c),
                     lhsT=w_codes[a][:, P * c : P * (c + 1)].bitcast(FP8X4),
                     lhsT_scale=w_scales[a][:, P * c : P * (c + 1)],
-                    rhs=picked(a, P * i, P * i + H),
-                    rhs_scale=g_planes[4 * a : P, P * i : P * i + H],
-                    start=(a == 0 and c % 2 == 0),
-                    stop=(a == PASSES - 1 and c % 2 == 1),
+                    rhs=picked(a, P * i, P * i + width),
+                    rhs_scale=g_planes[4 * a : P, P * i : P * i + width],
+                    start=(a == 0 and width * c % N == 0),
+                    stop=(a == PASSES - 1 and width * (c + 1) % N == 0),
                 )
 
-        def activate_turned(accs, i):
-            active = keep.tile([P, 4, H], F32, align_bytes=64, name=f"active{i}")
+        def activate_turned(accs, active):
             for c in range(4):
-                nc.scalar.activation(
-                    active[:, c], accs[c // 2][:, H * (c % 2) : H * (c % 2 + 1)], GELU, bias=bias_col[:, c : c + 1]
-                )
+                nc.scalar.activation(active[:, c], chunk_of(accs, c), GELU, bias=bias_col[:, c : c + 1])
             return active
 
         def turn_back(active, u, k):
@@ -119,20 +123,26 @@ def tile_list_tabw_tm_gelu_kernel(tc, tab, w, b, offs, out):
             nc.scalar.copy(result[:], back[:])
             nc.sync.dma_start(out=out[P * i : P * (i + 1), :], in_=result[:])
 
-        def finish(acc, i, parts=((0, N),)):
-            for n0, n1 in parts:
-                summed = laid.tile([P, n1 - n0], F32, align_bytes=64, offset=90112 + 2048 * i + 4 * n0, name=f"summed{i}_{n0}")
-                result = keep.tile([P, n1 - n0], F32, align_bytes=64, name=f"result{i}_{n0}")
-                nc.vector.tensor_tensor(summed[:], acc[:, n0:n1], bias[:, n0:n1], ADD)
-                nc.scalar.activation(result[:], summed[:], GELU)
-                nc.sync.dma_start(out=out[P * i : P * (i + 1), n0:n1], in_=result[:])
+        def finish(acc, i, parts=1, stores=1, second=None):
+            summed = laid.tile([P, N], F32, align_bytes=64, offset=90112 + 2048 * i + (2048 if i > 3 else 0), name=f"summed{i}")
+            result = keep.tile([P, N], F32, align_bytes=64, name=f"result{i}")
+            for part in range(parts):
+                cols = slice(N // parts * part, N // parts * (part + 1))
+                source = second if second is not None and part == 1 else acc
+                nc.vector.tensor_tensor(summed[:, cols], source[:, cols], bias[:, cols], ADD)
+                nc.scalar.activation(result[:, cols], summed[:, cols], GELU)
+                if stores == parts:
+                    nc.sync.dma_start(out=out[P * i : P * (i + 1), cols], in_=result[:, cols])
+            if stores != parts:
+                nc.sync.dma_start(out=out[P * i : P * (i + 1), :], in_=result[:])
 
         nc.vector.memset(planes[:].bitcast(I32), 0)
         nc.gpsimd.memset(warm[:], 0.0)
         nc.sync.dma_start(offsets[:], offs)
         load_words(0, keep.tile([P, T], I32, align_bytes=64, name="words0"))
-        nc.sync.dma_start(out=b_rows[:, 0:4], in_=b.rearrange("(p c) -> p c", c=4))
+        nc.sync.dma_start(out=b_rows[:], in_=b.rearrange("(p c) -> p c", c=4))
         raw0 = load_w(0, 40896)
+        raw1 = load_w(1, 16384)
         make_identity(nc, ident[:])
         scale_rows = tab[:, 512 * T : 528 * T].rearrange("a (q t) -> a q t", t=T)
         for quad in range(4):
@@ -150,43 +160,47 @@ def tile_list_tabw_tm_gelu_kernel(tc, tab, w, b, offs, out):
             nc.tensor.transpose(upright[:, P * c : P * (c + 1)], bias[:, P * c : P * (c + 1)], ident[:])
         nc.scalar.copy(bias_col[:], upright[:, 0:N:P])
         load_words(1, laid.tile([P, T], I32, align_bytes=64, offset=0, name="words1"))
-        raw1 = load_w(1, 16384)
 
         gather_words(0, 0, S, 73728)
         nc.vector.tensor_copy(g_planes[:], planes[:].indirect(offsets[:]))
         quantise(raw0, 0, 63488)
+        quantise(raw1, 1, 126976)
         raw2 = load_w(2, 49024)
         load_words(2, laid.tile([P, T], I32, align_bytes=64, offset=24576, name="words2"))
-        gather_words(1, 0, 512, 59392)
-        gather_words(1, 1024, 1536, 61440)
-        quantise(raw1, 1, 86016)
-        gather_words(1, 1536, S, 86016)
-        gather_words(1, 512, 1024, 88064)
+        gather_words(1, 0, 512, 61440)
+        gather_words(1, 1024, S, 126976 + 4096 - 64)
+        gather_words(1, 512, 1024, 126976)
         quantise(raw2, 2, 67584)
         accs = [bank(k) for k in range(BANKS)]
         for a in range(PASSES):
             if a == PASSES - 1:
                 gather_words(2, 0, 512, 81920)
                 gather_words(2, 512, 1024, 83968)
-            multiply_turned(accs, 0, a)
-            for i in range(2, BANKS):
+            multiply_turned(accs[0:2], 0, a)
+            multiply(accs[3], 3, a)
+            multiply_turned(accs[2:3], 2, a)
+            for i in range(4, BANKS):
                 multiply(accs[i], i, a)
-        active = activate_turned(accs, 0)
-        finish(accs[2], 2)
+        wide = activate_turned(accs[0:2], keep.tile([P, 4, 2 * P], F32, align_bytes=64, name="wide"))
         finish(accs[3], 3)
-        for u in range(2):
-            copy_out(turn_back(active, u, u), u)
+        narrow = laid.tile([P, 4, P], F32, align_bytes=64, offset=90112 + 2048 * 2 + 64, name="narrow")
+        activate_turned(accs[2:3], narrow)
         finish(accs[4], 4)
+        copy_out(turn_back(wide, 0, 0), 0)
         finish(accs[5], 5)
-        gather_words(2, 1024, 1536, 90112 + 2048 * 2)
+        gather_words(2, 1024, 1536, 90112 + 2048 * 3 + 64)
+        copy_out(turn_back(wide, 1, 1), 1)
         finish(accs[6], 6)
+        copy_out(turn_back(narrow, 0, 2), 2)
         finish(accs[7], 7)
-        gather_words(2, 1536, S, 90112 + 2048 * 5)
-        for first, banks in ((8, (2, 3, 4, 5)), (12, (0, 1, 6, 7))):
-            late = [bank(k) for k in banks]
-            for u in range(4):
-                for a in range(PASSES - 1):
-                    multiply(late[u], first + u, a)
-            for u in range(4):
-                multiply(late[u], first + u, PASSES - 1)
-                finish(late[u], first + u, ((0, N),) if first + u < TILES - 1 else ((0, H), (H, N)))
+        gather_words(2, 1536, S, 90112 + 2048 * 6)
+        for i, k in zip(range(BANKS, TILES - 1), (3, 4, 5, 0, 6, 7, 1)):
+            acc = bank(k)
+            for a in range(PASSES):
+                multiply(acc, i, a)
+            finish(acc, i, 1 if i < TILES - 2 else 2)
+        halves = [bank(2), bank(3)]
+        for h in range(2):
+            for a in range(PASSES):
+                multiply(halves[h], TILES - 1, a, slice(H * h, H * (h + 1)))
+        finish(halves[0], TILES - 1, 2, 2, halves[1])

@@ -32,15 +32,14 @@ def tile_list_tabw_tm_gelu_kernel(tc, tab, w, b, offs, out):
         offsets = keep.tile([P, S // 16], U16, name="offsets")
         planes = laid.tile([P, T], U8, align_bytes=64, offset=59328, name="planes")
         w_codes = [laid.tile([P, N], U32, align_bytes=64, offset=57344, name="w_codes0")]
-        w_codes.append(laid.tile([P, N], U32, align_bytes=64, offset=59392, name="w_codes1"))
-        w_codes.append(keep.tile([P, N], U32, align_bytes=64, name="w_codes2"))
+        w_codes.extend(keep.tile([P, N], U32, align_bytes=64, name=f"w_codes{a}") for a in range(1, PASSES))
         w_scales = [keep.tile([P, N], U8, align_bytes=64, name=f"w_scales{a}") for a in range(PASSES)]
         g_planes = keep.tile([P, S], U8, align_bytes=64, name="g_planes")
         bias = keep.tile([P, N], F32, align_bytes=64, name="bias")
         bias_col = keep.tile([P, 4], F32, align_bytes=64, name="bias_col")
         warm = keep.tile([P, 1], F32, name="warm")
         ident = keep.tile([P, P], F32, align_bytes=64, name="ident")
-        b_rows = laid.tile([P, 4], F32, align_bytes=64, offset=0, name="b_rows")
+        b_rows = laid.tile([P, 32], F32, align_bytes=64, offset=16384 - 64, name="b_rows")
         words = {}
         runs = {}
 
@@ -140,9 +139,8 @@ def tile_list_tabw_tm_gelu_kernel(tc, tab, w, b, offs, out):
         nc.gpsimd.memset(warm[:], 0.0)
         nc.sync.dma_start(offsets[:], offs)
         load_words(0, keep.tile([P, T], I32, align_bytes=64, name="words0"))
-        nc.sync.dma_start(out=b_rows[:], in_=b.rearrange("(p c) -> p c", c=4))
+        nc.sync.dma_start(out=b_rows[:, 0:4], in_=b.rearrange("(p c) -> p c", c=4))
         raw0 = load_w(0, 40896)
-        raw1 = load_w(1, 16384)
         make_identity(nc, ident[:])
         scale_rows = tab[:, 512 * T : 528 * T].rearrange("a (q t) -> a q t", t=T)
         for quad in range(4):
@@ -160,16 +158,18 @@ def tile_list_tabw_tm_gelu_kernel(tc, tab, w, b, offs, out):
             nc.tensor.transpose(upright[:, P * c : P * (c + 1)], bias[:, P * c : P * (c + 1)], ident[:])
         nc.scalar.copy(bias_col[:], upright[:, 0:N:P])
         load_words(1, laid.tile([P, T], I32, align_bytes=64, offset=0, name="words1"))
+        raw1 = load_w(1, 16384)
 
         gather_words(0, 0, S, 73728)
         nc.vector.tensor_copy(g_planes[:], planes[:].indirect(offsets[:]))
         quantise(raw0, 0, 63488)
-        quantise(raw1, 1, 126976)
         raw2 = load_w(2, 49024)
         load_words(2, laid.tile([P, T], I32, align_bytes=64, offset=24576, name="words2"))
-        gather_words(1, 0, 512, 61440)
-        gather_words(1, 1024, S, 126976 + 4096 - 64)
-        gather_words(1, 512, 1024, 126976)
+        gather_words(1, 0, 512, 59392)
+        gather_words(1, 1024, 1536, 61440)
+        quantise(raw1, 1, 86016)
+        gather_words(1, 1536, S, 86016)
+        gather_words(1, 512, 1024, 88064)
         quantise(raw2, 2, 67584)
         accs = [bank(k) for k in range(BANKS)]
         for a in range(PASSES):

@@ -16,10 +16,29 @@ GELU = mybir.ActivationFunctionType.Gelu_apprx_tanh
 K, N, T, S = 1536, 512, 4096, 2048
 P = 128
 PASSES = K // 512
-H = N // 2
+LAST_PASS = PASSES - 1
 TILES = S // P
 BANKS = 8
+CHUNKS = N // P
+QUARTER = S // 4
 FLOPS = 2 * K * N * S
+
+WORDS_BYTES, RAW_BYTES, ROW_BYTES = 4 * T, 16 * N, 4 * N
+AT_WORDS1 = 0
+AT_RAW1 = AT_WORDS1 + WORDS_BYTES
+AT_B_ROWS = AT_RAW1 - 64
+AT_WORDS2 = AT_RAW1 + RAW_BYTES
+AT_RAW0 = AT_WORDS2 + WORDS_BYTES - 256
+AT_RAW2 = AT_RAW0 + RAW_BYTES - 256
+AT_CODES0 = 56 * 1024
+AT_PLANES = AT_CODES0 + ROW_BYTES - 64
+AT_PICKED1_LATE = AT_CODES0 + ROW_BYTES
+AT_GROUPED0 = AT_PICKED1_LATE + 2 * ROW_BYTES
+AT_GROUPED2 = AT_GROUPED0 + 2 * ROW_BYTES
+AT_PICKED0 = AT_GROUPED2 + 3 * ROW_BYTES
+AT_PICKED2 = AT_PICKED0 + 4 * ROW_BYTES
+AT_GROUPED1 = AT_PICKED2 + 2 * ROW_BYTES
+AT_SUMMED = AT_GROUPED1 + 2 * ROW_BYTES
 
 
 def tile_list_tabw_tm_gelu_kernel(tc, tab, w, b, offs, out):
@@ -30,16 +49,15 @@ def tile_list_tabw_tm_gelu_kernel(tc, tab, w, b, offs, out):
         psum = ctx.enter_context(tc.psum_pool(name="psum", bufs=1))
 
         offsets = keep.tile([P, S // 16], U16, name="offsets")
-        planes = laid.tile([P, T], U8, align_bytes=64, offset=59328, name="planes")
-        w_codes = [laid.tile([P, N], U32, align_bytes=64, offset=57344, name="w_codes0")]
+        planes = laid.tile([P, T], U8, align_bytes=64, offset=AT_PLANES, name="planes")
+        w_codes = [laid.tile([P, N], U32, align_bytes=64, offset=AT_CODES0, name="w_codes0")]
         w_codes.extend(keep.tile([P, N], U32, align_bytes=64, name=f"w_codes{a}") for a in range(1, PASSES))
         w_scales = [keep.tile([P, N], U8, align_bytes=64, name=f"w_scales{a}") for a in range(PASSES)]
         g_planes = keep.tile([P, S], U8, align_bytes=64, name="g_planes")
         bias = keep.tile([P, N], F32, align_bytes=64, name="bias")
-        bias_col = keep.tile([P, 4], F32, align_bytes=64, name="bias_col")
-        warm = keep.tile([P, 1], F32, name="warm")
+        bias_col = keep.tile([P, CHUNKS], F32, align_bytes=64, name="bias_col")
         ident = keep.tile([P, P], F32, align_bytes=64, name="ident")
-        b_rows = laid.tile([P, 32], F32, align_bytes=64, offset=16384 - 64, name="b_rows")
+        b_rows = laid.tile([P, 32], F32, align_bytes=64, offset=AT_B_ROWS, name="b_rows")
         words = {}
         runs = {}
 
@@ -51,7 +69,7 @@ def tile_list_tabw_tm_gelu_kernel(tc, tab, w, b, offs, out):
             nc.sync.dma_start(out=tile[:], in_=tab[a, 0 : 512 * T].rearrange("(p x) -> p x", p=P).bitcast(I32))
 
         def load_w(a, offset):
-            raw = laid.tile([P, 4, N], F32, align_bytes=64, offset=offset, name=f"w_raw{a}")
+            raw = laid.tile([P, 4, N], F32, align_bytes=256, offset=offset, name=f"w_raw{a}")
             nc.sync.dma_start(out=raw[:], in_=w[512 * a : 512 * (a + 1), :].rearrange("(p j) n -> p j n", j=4))
             return raw
 
@@ -85,62 +103,59 @@ def tile_list_tabw_tm_gelu_kernel(tc, tab, w, b, offs, out):
                 rhs=w_codes[a][:, cols].bitcast(FP8X4),
                 rhs_scale=w_scales[a][:, cols],
                 start=(a == 0),
-                stop=(a == PASSES - 1),
+                stop=(a == LAST_PASS),
             )
 
-        def chunk_of(accs, c):
-            width = P * len(accs)
+        def chunk_of(banks, c):
+            width = P * len(banks)
             first = width * c % N
-            return accs[width * c // N][:, first : first + width]
+            return banks[width * c // N][:, first : first + width]
 
-        def multiply_turned(accs, i, a):
-            width = P * len(accs)
-            for c in range(4):
+        def multiply_turned(banks, i, a):
+            width = P * len(banks)
+            for c in range(CHUNKS):
                 nc.tensor.matmul_mx(
-                    out=chunk_of(accs, c),
+                    out=chunk_of(banks, c),
                     lhsT=w_codes[a][:, P * c : P * (c + 1)].bitcast(FP8X4),
                     lhsT_scale=w_scales[a][:, P * c : P * (c + 1)],
                     rhs=picked(a, P * i, P * i + width),
                     rhs_scale=g_planes[4 * a : P, P * i : P * i + width],
                     start=(a == 0 and width * c % N == 0),
-                    stop=(a == PASSES - 1 and width * (c + 1) % N == 0),
+                    stop=(a == LAST_PASS and width * (c + 1) % N == 0),
                 )
 
-        def activate_turned(accs, active):
-            for c in range(4):
-                nc.scalar.activation(active[:, c], chunk_of(accs, c), GELU, bias=bias_col[:, c : c + 1])
+        def activate_turned(banks, name):
+            active = keep.tile([P, CHUNKS, P * len(banks)], F32, align_bytes=64, name=name)
+            for c in range(CHUNKS):
+                nc.scalar.activation(active[:, c], chunk_of(banks, c), GELU, bias=bias_col[:, c : c + 1])
             return active
 
-        def turn_back(active, u, k):
-            back = bank(k)
-            for c in range(4):
+        def finish_turned(active, u, i):
+            back = bank(i)
+            for c in range(CHUNKS):
                 nc.tensor.transpose(back[:, P * c : P * (c + 1)], active[:, c, P * u : P * (u + 1)], ident[:])
-            return back
-
-        def copy_out(back, i):
-            result = keep.tile([P, N], F32, align_bytes=64, name=f"result{i}")
+            result = keep.tile([P, N], F32, align_bytes=256, name=f"result{i}")
             nc.scalar.copy(result[:], back[:])
             nc.sync.dma_start(out=out[P * i : P * (i + 1), :], in_=result[:])
 
-        def finish(acc, i, parts=1, stores=1, second=None):
-            summed = laid.tile([P, N], F32, align_bytes=64, offset=90112 + 2048 * i + (2048 if i > 3 else 0), name=f"summed{i}")
-            result = keep.tile([P, N], F32, align_bytes=64, name=f"result{i}")
-            for part in range(parts):
-                cols = slice(N // parts * part, N // parts * (part + 1))
-                source = second if second is not None and part == 1 else acc
+        def finish(sources, i, store_parts=False):
+            summed = laid.tile([P, N], F32, align_bytes=64, offset=AT_SUMMED + ROW_BYTES * i, name=f"summed{i}")
+            result = keep.tile([P, N], F32, align_bytes=256, name=f"result{i}")
+            width = N // len(sources)
+            for h, source in enumerate(sources):
+                cols = slice(width * h, width * (h + 1))
                 nc.vector.tensor_tensor(summed[:, cols], source[:, cols], bias[:, cols], ADD)
                 nc.scalar.activation(result[:, cols], summed[:, cols], GELU)
-                if stores == parts:
+                if store_parts:
                     nc.sync.dma_start(out=out[P * i : P * (i + 1), cols], in_=result[:, cols])
-            if stores != parts:
+            if not store_parts:
                 nc.sync.dma_start(out=out[P * i : P * (i + 1), :], in_=result[:])
 
         nc.vector.memset(planes[:].bitcast(I32), 0)
-        nc.gpsimd.memset(warm[:], 0.0)
+        load_words(0, keep.tile([P, T], I32, align_bytes=256, name="words0"))
         nc.sync.dma_start(offsets[:], offs)
-        load_words(0, keep.tile([P, T], I32, align_bytes=64, name="words0"))
         nc.sync.dma_start(out=b_rows[:, 0:4], in_=b.rearrange("(p c) -> p c", c=4))
-        raw0 = load_w(0, 40896)
+        raw0 = load_w(0, AT_RAW0)
         make_identity(nc, ident[:])
         scale_rows = tab[:, 512 * T : 528 * T].rearrange("a (q t) -> a q t", t=T)
         for quad in range(4):
@@ -148,59 +163,66 @@ def tile_list_tabw_tm_gelu_kernel(tc, tab, w, b, offs, out):
                 out=planes[32 * quad : 32 * quad + 4 * PASSES, :].bitcast(I32),
                 in_=scale_rows[:, 4 * quad : 4 * quad + 4, :].bitcast(I32),
             )
-        nc.scalar.activation(warm[:], warm[:], GELU)
         spread = bank(0)
         for c in range(4):
             nc.tensor.transpose(spread[:, P * c : P * (c + 1)], b_rows[:, c : c + 1].to_broadcast([P, P]), ident[:])
         nc.scalar.copy(bias[:].rearrange("p (m c) -> p m c", c=4), spread[:].rearrange("p (c m) -> p m c", c=4))
         upright = bank(1)
-        for c in range(4):
+        for c in range(CHUNKS):
             nc.tensor.transpose(upright[:, P * c : P * (c + 1)], bias[:, P * c : P * (c + 1)], ident[:])
         nc.scalar.copy(bias_col[:], upright[:, 0:N:P])
-        load_words(1, laid.tile([P, T], I32, align_bytes=64, offset=0, name="words1"))
-        raw1 = load_w(1, 16384)
+        load_words(1, laid.tile([P, T], I32, align_bytes=64, offset=AT_WORDS1, name="words1"))
+        raw1 = load_w(1, AT_RAW1)
 
-        gather_words(0, 0, S, 73728)
+        gather_words(0, 0, S, AT_PICKED0)
         nc.vector.tensor_copy(g_planes[:], planes[:].indirect(offsets[:]))
-        quantise(raw0, 0, 63488)
-        raw2 = load_w(2, 49024)
-        load_words(2, laid.tile([P, T], I32, align_bytes=64, offset=24576, name="words2"))
-        gather_words(1, 0, 512, 59392)
-        gather_words(1, 1024, 1536, 61440)
-        quantise(raw1, 1, 86016)
-        gather_words(1, 1536, S, 86016)
-        gather_words(1, 512, 1024, 88064)
-        quantise(raw2, 2, 67584)
+        quantise(raw0, 0, AT_GROUPED0)
+        raw2 = load_w(2, AT_RAW2)
+        load_words(2, laid.tile([P, T], I32, align_bytes=64, offset=AT_WORDS2, name="words2"))
+        gather_words(1, 2 * QUARTER, S, AT_PICKED1_LATE)
+        quantise(raw1, 1, AT_GROUPED1)
+        for q in range(2):
+            gather_words(1, QUARTER * q, QUARTER * (q + 1), AT_GROUPED1 + ROW_BYTES * q)
+        quantise(raw2, 2, AT_GROUPED2)
+
         accs = [bank(k) for k in range(BANKS)]
         for a in range(PASSES):
-            if a == PASSES - 1:
-                gather_words(2, 0, 512, 81920)
-                gather_words(2, 512, 1024, 83968)
+            if a == LAST_PASS:
+                for q in range(2):
+                    gather_words(a, QUARTER * q, QUARTER * (q + 1), AT_PICKED2 + ROW_BYTES * q)
             multiply_turned(accs[0:2], 0, a)
             multiply(accs[3], 3, a)
             multiply_turned(accs[2:3], 2, a)
             for i in range(4, BANKS):
                 multiply(accs[i], i, a)
-        wide = activate_turned(accs[0:2], keep.tile([P, 4, 2 * P], F32, align_bytes=64, name="wide"))
-        finish(accs[3], 3)
-        narrow = laid.tile([P, 4, P], F32, align_bytes=64, offset=90112 + 2048 * 2 + 64, name="narrow")
-        activate_turned(accs[2:3], narrow)
-        finish(accs[4], 4)
-        copy_out(turn_back(wide, 0, 0), 0)
-        finish(accs[5], 5)
-        gather_words(2, 1024, 1536, 90112 + 2048 * 3 + 64)
-        copy_out(turn_back(wide, 1, 1), 1)
-        finish(accs[6], 6)
-        copy_out(turn_back(narrow, 0, 2), 2)
-        finish(accs[7], 7)
-        gather_words(2, 1536, S, 90112 + 2048 * 6)
-        for i, k in zip(range(BANKS, TILES - 1), (3, 4, 5, 0, 6, 7, 1)):
-            acc = bank(k)
+        pair = activate_turned(accs[0:2], "pair")
+        single = activate_turned(accs[2:3], "single")
+        finish([accs[3]], 3)
+        finish([accs[4]], 4)
+        finish_turned(pair, 0, 0)
+        finish([accs[5]], 5)
+        finish_turned(pair, 1, 1)
+        finish([accs[6]], 6)
+        gather_words(LAST_PASS, 2 * QUARTER, 3 * QUARTER, AT_SUMMED + ROW_BYTES * 3)
+        finish_turned(single, 0, 2)
+        finish([accs[7]], 7)
+        gather_words(LAST_PASS, 3 * QUARTER, S, AT_SUMMED + ROW_BYTES * 5)
+
+        freed = (3, 4, 5, 6, 0, 7, 1)
+        early = [bank(k) for k in freed[:3]]
+        for u, acc in enumerate(early):
+            for a in range(LAST_PASS):
+                multiply(acc, BANKS + u, a)
+        for u, acc in enumerate(early):
+            multiply(acc, BANKS + u, LAST_PASS)
+            finish([acc], BANKS + u)
+        for u in range(len(early), len(freed)):
+            acc = bank(freed[u])
             for a in range(PASSES):
-                multiply(acc, i, a)
-            finish(acc, i, 1 if i < TILES - 2 else 2)
+                multiply(acc, BANKS + u, a)
+            finish([acc] if u < len(freed) - 1 else [acc, acc], BANKS + u)
         halves = [bank(2), bank(3)]
-        for h in range(2):
+        for h, acc in enumerate(halves):
             for a in range(PASSES):
-                multiply(halves[h], TILES - 1, a, slice(H * h, H * (h + 1)))
-        finish(halves[0], TILES - 1, 2, 2, halves[1])
+                multiply(acc, TILES - 1, a, slice(N // 2 * h, N // 2 * (h + 1)))
+        finish(halves, TILES - 1, store_parts=True)

@@ -33,7 +33,7 @@ AT_RAW2 = AT_RAW0 + RAW_BYTES - 256
 AT_CODES0 = 56 * 1024
 AT_PLANES = AT_CODES0 + ROW_BYTES - 64
 AT_PICKED1_LATE = AT_CODES0 + ROW_BYTES
-AT_GROUPED0 = AT_PICKED1_LATE + 2 * ROW_BYTES
+AT_GROUPED0 = AT_PICKED1_LATE + 3 * ROW_BYTES
 AT_GROUPED2 = AT_GROUPED0 + 2 * ROW_BYTES
 AT_PICKED0 = AT_GROUPED2 + 3 * ROW_BYTES
 AT_PICKED2 = AT_PICKED0 + 4 * ROW_BYTES
@@ -147,7 +147,7 @@ def tile_list_tabw_tm_gelu_kernel(tc, tab, w, b, offs, out):
                 nc.vector.tensor_tensor(summed[:, cols], source[:, cols], bias[:, cols], ADD)
                 nc.scalar.activation(result[:, cols], summed[:, cols], GELU)
                 if store_parts:
-                    nc.sync.dma_start(out=out[P * i : P * (i + 1), cols], in_=result[:, cols])
+                    (nc.scalar if h == 1 else nc.sync).dma_start(out=out[P * i : P * (i + 1), cols], in_=result[:, cols])
             if not store_parts:
                 nc.sync.dma_start(out=out[P * i : P * (i + 1), :], in_=result[:])
 
@@ -179,10 +179,9 @@ def tile_list_tabw_tm_gelu_kernel(tc, tab, w, b, offs, out):
         quantise(raw0, 0, AT_GROUPED0)
         raw2 = load_w(2, AT_RAW2)
         load_words(2, laid.tile([P, T], I32, align_bytes=64, offset=AT_WORDS2, name="words2"))
-        gather_words(1, 2 * QUARTER, S, AT_PICKED1_LATE)
+        gather_words(1, QUARTER, S, AT_PICKED1_LATE)
         quantise(raw1, 1, AT_GROUPED1)
-        for q in range(2):
-            gather_words(1, QUARTER * q, QUARTER * (q + 1), AT_GROUPED1 + ROW_BYTES * q)
+        gather_words(1, 0, QUARTER, AT_GROUPED1)
         quantise(raw2, 2, AT_GROUPED2)
 
         accs = [bank(k) for k in range(BANKS)]

@@ -171,16 +171,16 @@ def tile_list_tabw_tm_gelu_kernel(tc, tab, w, b, offs, out):
         for c in range(CHUNKS):
             nc.tensor.transpose(upright[:, P * c : P * (c + 1)], bias[:, P * c : P * (c + 1)], ident[:])
         nc.scalar.copy(bias_col[:], upright[:, 0:N:P])
-        load_words(1, laid.tile([P, T], I32, align_bytes=64, offset=AT_WORDS1, name="words1"))
         raw1 = load_w(1, AT_RAW1)
+        load_words(1, laid.tile([P, T], I32, align_bytes=64, offset=AT_WORDS1, name="words1"))
 
         gather_words(0, 0, S, AT_PICKED0)
         nc.vector.tensor_copy(g_planes[:], planes[:].indirect(offsets[:]))
         quantise(raw0, 0, AT_GROUPED0)
         raw2 = load_w(2, AT_RAW2)
         load_words(2, laid.tile([P, T], I32, align_bytes=64, offset=AT_WORDS2, name="words2"))
-        gather_words(1, QUARTER, S, AT_PICKED1_LATE)
         quantise(raw1, 1, AT_GROUPED1)
+        gather_words(1, QUARTER, S, AT_PICKED1_LATE)
         gather_words(1, 0, QUARTER, AT_GROUPED1)
         quantise(raw2, 2, AT_GROUPED2)
 
@@ -219,7 +219,7 @@ def tile_list_tabw_tm_gelu_kernel(tc, tab, w, b, offs, out):
             acc = bank(freed[u])
             for a in range(PASSES):
                 multiply(acc, BANKS + u, a)
-            finish([acc] if u < len(freed) - 1 else [acc, acc], BANKS + u)
+            finish([acc], BANKS + u)
         halves = [bank(2), bank(3)]
         for h, acc in enumerate(halves):
             for a in range(PASSES):

from contextlib import ExitStack

import concourse.mybir as mybir
from concourse.masks import make_identity

F32 = mybir.dt.float32
BF16 = mybir.dt.bfloat16
I32 = mybir.dt.int32
U32 = mybir.dt.uint32
U16 = mybir.dt.uint16
U8 = mybir.dt.uint8
FP8X4 = mybir.dt.float8_e4m3fn_x4
ADD = mybir.AluOpType.add
GELU = mybir.ActivationFunctionType.Gelu_apprx_tanh

K, N, T, S = 1536, 512, 4096, 2048
P = 128
PASSES = K // 512
LAST_PASS = PASSES - 1
TILES = S // P
BANKS = 8
CHUNKS = N // P
QUARTER = S // 4
FLOPS = 2 * K * N * S

WORDS_BYTES, RAW_BYTES, ROW_BYTES = 4 * T, 16 * N, 4 * N
AT_WORDS1 = 0
AT_RAW1 = AT_WORDS1 + WORDS_BYTES
AT_B_ROWS = AT_RAW1 - 64
AT_WORDS2 = AT_RAW1 + RAW_BYTES
AT_RAW0 = AT_WORDS2 + WORDS_BYTES - 256
AT_RAW2 = AT_RAW0 + RAW_BYTES - 256
AT_CODES0 = 56 * 1024
AT_PLANES = AT_CODES0 + ROW_BYTES - 64
AT_PICKED1_LATE = AT_CODES0 + ROW_BYTES
AT_GROUPED0 = AT_PICKED1_LATE + 3 * ROW_BYTES
AT_GROUPED2 = AT_GROUPED0 + 2 * ROW_BYTES
AT_PICKED0 = AT_GROUPED2 + 3 * ROW_BYTES
AT_PICKED2 = AT_PICKED0 + 4 * ROW_BYTES
AT_GROUPED1 = AT_PICKED2 + 2 * ROW_BYTES
AT_SUMMED = AT_GROUPED1 + 2 * ROW_BYTES


def tile_list_tabw_tm_gelu_kernel(tc, tab, w, b, offs, out):
    nc = tc.nc
    with ExitStack() as ctx:
        keep = ctx.enter_context(tc.tile_pool(name="keep", bufs=1))
        laid = ctx.enter_context(tc.tile_pool(name="laid", bufs=1))
        psum = ctx.enter_context(tc.psum_pool(name="psum", bufs=1))

        offsets = keep.tile([P, S // 16], U16, name="offsets")
        planes = laid.tile([P, T], U8, align_bytes=64, offset=AT_PLANES, name="planes")
        w_codes = [laid.tile([P, N], U32, align_bytes=64, offset=AT_CODES0, name="w_codes0")]
        w_codes.extend(keep.tile([P, N], U32, align_bytes=64, name=f"w_codes{a}") for a in range(1, PASSES))
        w_scales = [keep.tile([P, N], U8, align_bytes=64, name=f"w_scales{a}") for a in range(PASSES)]
        g_planes = keep.tile([P, S], U8, align_bytes=64, name="g_planes")
        bias = keep.tile([P, N], F32, align_bytes=64, name="bias")
        bias_col = keep.tile([P, CHUNKS], F32, align_bytes=64, name="bias_col")
        ident = keep.tile([P, P], F32, align_bytes=64, name="ident")
        b_rows = laid.tile([P, 32], F32, align_bytes=64, offset=AT_B_ROWS, name="b_rows")
        words = {}
        runs = {}

        def bank(k):
            return psum.tile([P, N], F32, name=f"bank{k}")

        def load_words(a, tile):
            words[a] = tile
            nc.sync.dma_start(out=tile[:], in_=tab[a, 0 : 512 * T].rearrange("(p x) -> p x", p=P).bitcast(I32))

        def load_w(a, offset):
            raw = laid.tile([P, 4, N], F32, align_bytes=256, offset=offset, name=f"w_raw{a}")
            nc.sync.dma_start(out=raw[:], in_=w[512 * a : 512 * (a + 1), :].rearrange("(p j) n -> p j n", j=4))
            return raw

        def quantise(raw, a, offset):
            grouped = laid.tile([P, N, 4], BF16, align_bytes=64, offset=offset, name=f"w_grp{a}")
            nc.scalar.copy(
                grouped[:].rearrange("p (c i) t -> p c t i", i=4),
                raw[:].rearrange("p t (c i) -> p c t i", i=4),
            )
            nc.vector.quantize_mx(
                out=w_codes[a][:].bitcast(FP8X4),
                scales=w_scales[a][:],
                in_=grouped[:].rearrange("p n t -> p (n t)"),
            )

        def gather_words(a, j0, j1, offset):
            tile = laid.tile([P, j1 - j0], U32, align_bytes=64, offset=offset, name=f"picked{a}_{j0}")
            nc.vector.tensor_copy(tile[:], words[a][:].bitcast(U32).indirect(offsets[:, j0 // 16 : j1 // 16]))
            for i in range(j0 // P, j1 // P):
                runs[(a, i)] = (tile, j0)

        def picked(a, j0, j1):
            tile, first = runs[(a, j0 // P)]
            return tile[:, j0 - first : j1 - first].bitcast(FP8X4)

        def multiply(acc, i, a, cols=slice(0, N)):
            nc.tensor.matmul_mx(
                out=acc[:, cols],
                lhsT=picked(a, P * i, P * (i + 1)),
                lhsT_scale=g_planes[4 * a : P, P * i : P * (i + 1)],
                rhs=w_codes[a][:, cols].bitcast(FP8X4),
                rhs_scale=w_scales[a][:, cols],
                start=(a == 0),
                stop=(a == LAST_PASS),
            )

        def chunk_of(banks, c):
            width = P * len(banks)
            first = width * c % N
            return banks[width * c // N][:, first : first + width]

        def multiply_turned(banks, i, a):
            width = P * len(banks)
            for c in range(CHUNKS):
                nc.tensor.matmul_mx(
                    out=chunk_of(banks, c),
                    lhsT=w_codes[a][:, P * c : P * (c + 1)].bitcast(FP8X4),
                    lhsT_scale=w_scales[a][:, P * c : P * (c + 1)],
                    rhs=picked(a, P * i, P * i + width),
                    rhs_scale=g_planes[4 * a : P, P * i : P * i + width],
                    start=(a == 0 and width * c % N == 0),
                    stop=(a == LAST_PASS and width * (c + 1) % N == 0),
                )

        def activate_turned(banks, name):
            active = keep.tile([P, CHUNKS, P * len(banks)], F32, align_bytes=64, name=name)
            for c in range(CHUNKS):
                nc.scalar.activation(active[:, c], chunk_of(banks, c), GELU, bias=bias_col[:, c : c + 1])
            return active

        def finish_turned(active, u, i):
            back = bank(i)
            for c in range(CHUNKS):
                nc.tensor.transpose(back[:, P * c : P * (c + 1)], active[:, c, P * u : P * (u + 1)], ident[:])
            result = keep.tile([P, N], F32, align_bytes=256, name=f"result{i}")
            nc.scalar.copy(result[:], back[:])
            nc.sync.dma_start(out=out[P * i : P * (i + 1), :], in_=result[:])

        def finish(sources, i, store_parts=False):
            summed = laid.tile([P, N], F32, align_bytes=64, offset=AT_SUMMED + ROW_BYTES * i, name=f"summed{i}")
            result = keep.tile([P, N], F32, align_bytes=256, name=f"result{i}")
            width = N // len(sources)
            for h, source in enumerate(sources):
                cols = slice(width * h, width * (h + 1))
                nc.vector.tensor_tensor(summed[:, cols], source[:, cols], bias[:, cols], ADD)
                nc.scalar.activation(result[:, cols], summed[:, cols], GELU)
                if store_parts:
                    (nc.scalar if h == 1 else nc.sync).dma_start(out=out[P * i : P * (i + 1), cols], in_=result[:, cols])
            if not store_parts:
                nc.sync.dma_start(out=out[P * i : P * (i + 1), :], in_=result[:])

        nc.vector.memset(planes[:].bitcast(I32), 0)
        load_words(0, keep.tile([P, T], I32, align_bytes=256, name="words0"))
        nc.sync.dma_start(offsets[:], offs)
        nc.sync.dma_start(out=b_rows[:, 0:4], in_=b.rearrange("(p c) -> p c", c=4))
        raw0 = load_w(0, AT_RAW0)
        make_identity(nc, ident[:])
        scale_rows = tab[:, 512 * T : 528 * T].rearrange("a (q t) -> a q t", t=T)
        for quad in range(4):
            nc.gpsimd.dma_start(
                out=planes[32 * quad : 32 * quad + 4 * PASSES, :].bitcast(I32),
                in_=scale_rows[:, 4 * quad : 4 * quad + 4, :].bitcast(I32),
            )
        spread = bank(0)
        for c in range(4):
            nc.tensor.transpose(spread[:, P * c : P * (c + 1)], b_rows[:, c : c + 1].to_broadcast([P, P]), ident[:])
        nc.scalar.copy(bias[:].rearrange("p (m c) -> p m c", c=4), spread[:].rearrange("p (c m) -> p m c", c=4))
        upright = bank(1)
        for c in range(CHUNKS):
            nc.tensor.transpose(upright[:, P * c : P * (c + 1)], bias[:, P * c : P * (c + 1)], ident[:])
        nc.scalar.copy(bias_col[:], upright[:, 0:N:P])
        raw1 = load_w(1, AT_RAW1)
        load_words(1, laid.tile([P, T], I32, align_bytes=64, offset=AT_WORDS1, name="words1"))

        gather_words(0, 0, S, AT_PICKED0)
        nc.vector.tensor_copy(g_planes[:], planes[:].indirect(offsets[:]))
        quantise(raw0, 0, AT_GROUPED0)
        raw2 = load_w(2, AT_RAW2)
        load_words(2, laid.tile([P, T], I32, align_bytes=64, offset=AT_WORDS2, name="words2"))
        quantise(raw1, 1, AT_GROUPED1)
        gather_words(1, QUARTER, S, AT_PICKED1_LATE)
        gather_words(1, 0, QUARTER, AT_GROUPED1)
        quantise(raw2, 2, AT_GROUPED2)

        accs = [bank(k) for k in range(BANKS)]
        for a in range(PASSES):
            if a == LAST_PASS:
                for q in range(2):
                    gather_words(a, QUARTER * q, QUARTER * (q + 1), AT_PICKED2 + ROW_BYTES * q)
            multiply_turned(accs[0:2], 0, a)
            multiply(accs[3], 3, a)
            multiply_turned(accs[2:3], 2, a)
            for i in range(4, BANKS):
                multiply(accs[i], i, a)
        pair = activate_turned(accs[0:2], "pair")
        single = activate_turned(accs[2:3], "single")
        finish([accs[3]], 3)
        finish([accs[4]], 4)
        finish_turned(pair, 0, 0)
        finish([accs[5]], 5)
        finish_turned(pair, 1, 1)
        finish([accs[6]], 6)
        gather_words(LAST_PASS, 2 * QUARTER, 3 * QUARTER, AT_SUMMED + ROW_BYTES * 3)
        finish_turned(single, 0, 2)
        finish([accs[7]], 7)
        gather_words(LAST_PASS, 3 * QUARTER, S, AT_SUMMED + ROW_BYTES * 5)

        freed = (3, 4, 5, 6, 0, 7, 1)
        early = [bank(k) for k in freed[:3]]
        for u, acc in enumerate(early):
            for a in range(LAST_PASS):
                multiply(acc, BANKS + u, a)
        for u, acc in enumerate(early):
            multiply(acc, BANKS + u, LAST_PASS)
            finish([acc], BANKS + u)
        for u in range(len(early), len(freed)):
            acc = bank(freed[u])
            for a in range(PASSES):
                multiply(acc, BANKS + u, a)
            finish([acc], BANKS + u)
        halves = [bank(2), bank(3)]
        for h, acc in enumerate(halves):
            for a in range(PASSES):
                multiply(acc, TILES - 1, a, slice(N // 2 * h, N // 2 * (h + 1)))
        finish(halves, TILES - 1, store_parts=True)
